import numpy as np, ml_dtypes
CORES = [51,54,179,182]
N = 4
BF = ml_dtypes.bfloat16
W, C, L, H, RO = 2048, 96, 384, 9, 5
ROW = np.arange(16)[:, None]
def parts(rng):
    z = (rng.integers(20, 257, (N, 8, 1, W)) * rng.random((N, 8, 16, W))).astype(np.int64)
    a = 1 + (rng.integers(10, 255, (N, 8, 1, L)) * rng.random((N, 8, 16, L))).astype(np.int64)
    w = rng.integers(0, 16, (N, 8, 16, 1)); e = rng.integers(0, W - 1, (N, 8, 16, L))
    often = np.take_along_axis(rng.integers(0, W - 1, (N, 8, 24)), rng.integers(0, 24, (N, 8, 16 * L)), 2).reshape(e.shape)
    e = np.where(rng.random(e.shape) < 0.1, often, e)
    n = rng.integers(2, 13, (N, 8, 1, L)); u = rng.random(n.shape)
    n = np.where(u < 0.04, 0, np.where(u < 0.07, 1, np.where(u < 0.11, 16, n)))
    return np.where(ROW < n, e, W - 1), a, z, w
def poor(rng, n):
    return np.where(np.argsort(rng.random((16, n)), axis=0) < 17 - H, 0, rng.integers(0, 256, (16, n)))
def pack(e, a, z, w):
    z[..., W - 1] = 0
    return {"bills": np.ascontiguousarray(e.reshape(N, 128, L)).astype(np.int32), "due": np.ascontiguousarray(a.reshape(N, 128, L)).astype(np.float32).astype(BF),
            "z0": np.ascontiguousarray(z.reshape(N, 128, W)).astype(np.float32).astype(BF), "wt": np.ascontiguousarray(w.reshape(N, 128, 1)).astype(np.float32).astype(BF)}
def setup_inputs(rng):
    return pack(*parts(rng))
def setup_inputs_room(rng):
    e, a, z, w = parts(rng); a = rng.integers(1, 41, a.shape); w[:, :, 0] = 1
    for q in range(N):
        for g in range(8):
            o = rng.permutation(W - 1); pay, b = o[:L], o[L:]
            z[q, g][:, b] = poor(rng, len(b)); z[q, g][:, pay] = rng.integers(64, 256, (16, L))
            n = np.full(N, C); d1, d2, d3 = (q + 1) % N, (q + 2) % N, (q + 3) % N
            if g % 4 == 0: n[d2] += 1; n[d3] -= 1
            if g % 4 == 1: n[:] = 0; n[d1] = L
            if g % 4 == 2: n[d1] -= 1; n[q] += 1
            if g % 4 == 3: n[d1] = 0; n[d2] += C
            to = rng.permutation(np.repeat(np.arange(N), n)); k = rng.integers(1, 15, L); top = k + rng.integers(0, 16 - k)
            e[q, g] = np.where(ROW < k, rng.integers(0, W - 1, (16, L)), np.where(ROW == k, pay, np.where(ROW <= top, b[rng.integers(0, len(b), (16, L))], W - 1)))
            s = np.sum(w[q, g] * (z[q, g][:, pay] - a[q, g]), axis=0)
            z[q, g, 0, pay] -= (s - to) % N
    return pack(e, a, z, w)
def setup_inputs_ties(rng):
    e, a, z, w = parts(rng); m = min(8, (W - 1) // L)
    for q in range(N):
        for g in range(8):
            o = rng.permutation(W - 1)[:L * m].reshape(m, L); x = a[q, g][:, None, :]
            n = rng.choice(np.array([0, H - 1, H - 1, H, H, H + 1]), (m, L)); good = np.argsort(rng.random((16, m, L)), axis=0) < n
            u = rng.random((16, m, L)); more = np.where(u < 0.5, 0, np.where(u < 0.65, 1, rng.integers(0, 256, u.shape)))
            if q == 0 and g == 0: more = more * 0
            v = np.where(good, np.minimum(x + more, 255), np.where(rng.random(u.shape) < 0.7, x - 1, 0))
            z[q, g][:, o.reshape(-1)] = v.reshape(16, -1)
            r = ROW - rng.integers(0, 17 - m, L)
            e[q, g] = np.where(r < 0, rng.integers(0, W - 1, (16, L)), np.where(r < m, np.take_along_axis(o, np.clip(r, 0, m - 1), 0), W - 1))
    return pack(e, a, z, w)
def setup_inputs_alike(rng):
    e, a, z, w = parts(rng); a = rng.integers(1, 21, a.shape)
    for q in range(N):
        for g in range(8):
            few = rng.permutation(W - 1)[:(1, 2, 3, 40)[g % 4]]
            if g % 4 == 1: few = np.array([0, W - 2])
            z[q, g][:, few] = rng.integers(160, 256, (16, len(few)))
            e[q, g] = np.where(e[q, g] == W - 1, W - 1, few[rng.integers(0, len(few), (16, L))])
    return pack(e, a, z, w)
def setup_inputs_ends(rng):
    e, a, z, w = parts(rng); a = rng.integers(1, 41, a.shape)
    w[:, 2] = 0; w[:, 3] = 15; w[:, 4] = 0; w[:, 4, :2] = 15; w[:, 4, 2] = 1
    xy = (W - 1) // 15 - 13; left = np.array([xy // 2, xy - xy // 2, W - 1 - 15 * xy])[:, None]; t = L // 4
    for q in range(N):
        for g in range(8):
            o = rng.permutation(W - 1); h, b = o[:W // 2], o[W // 2:]
            z[q, g][:, b] = poor(rng, len(b)); z[q, g][:, h] = rng.integers(128, 256, (16, len(h)))
            ri = h[rng.integers(8, len(h), (16, L))]; po = b[rng.integers(0, len(b), (16, L))]; no = np.full((16, L), W - 1)
            if g == 5:
                z[q, g][:, W - 2] = 200; z[q, g][:, 0] = 150
                u = rng.random((16, L)); ri = np.where(u < 0.1, W - 2, np.where(u < 0.2, 0, ri))
            kind = rng.integers(0, 9, L)[None, :]; some = rng.random((16, L)) < 0.3; one = rng.integers(1, 15, L)
            e[q, g] = np.choose(kind, [no, np.where(ROW == 0, ri, no), ri, np.where(ROW < 15, ri, po), np.where(ROW == 0, ri, po), np.where((ROW % 2 == 0) & (ROW < 14), ri, no),
                                       np.where((ROW > 0) & some, ri, no), np.where(ROW == one, ri, no), np.where((ROW == 15) | (ROW % 4 == 1), ri, no)])
            if g == 0:
                z[q, g][:, h[0]] = 255
                for j in range(2):
                    at = L - 8 + 4 * j; k = int(rng.integers(1, 15))
                    e[q, g][:, at:at + 4] = np.where(ROW < k, ri[:, :1], np.where(ROW == k, h[j], W - 1))
                    a[q, g][:, at:at + 4] = np.full((16, 1), 255) if j == 0 else rng.integers(1, 41, (16, 1))
            if g == 3 or g == 4:
                if g == 3: a[q, g][:, :t] = rng.integers(1, 21, (16, t)); z[q, g][:, h[:t]] = 255
                if g == 4: z[q, g][:3, h[:t]] = a[q, g][:3, :t] + left
                k = rng.integers(1, 15, t)
                e[q, g][:, :t] = np.where(ROW < k, h[rng.integers(t, len(h), (16, t))], np.where(ROW == k, h[:t], W - 1))
    e[:, rng.integers(6, 8)] = W - 1; e[rng.integers(0, N), 1] = W - 1
    return pack(e, a, z, w)
def setup_inputs_spread(rng):
    e, a, z, w = parts(rng)
    z = (np.exp2(8 * rng.random((N, 8, 1, W))) * rng.random(z.shape)).astype(np.int64)
    a = 1 + (np.exp2(7.9 * rng.random((N, 8, 1, L))) * rng.random(a.shape)).astype(np.int64)
    w = (16 * rng.random(w.shape) ** 3).astype(np.int64)
    e = np.where(e == W - 1, W - 1, np.minimum(((W - 1) * rng.random(e.shape) ** 2).astype(np.int64), W - 2))
    return pack(e, a, z, w)
def check_inputs(d):
    bad = []
    for k, lo, hi in (("bills", 0, W - 1), ("due", 1, 255), ("z0", 0, 255), ("wt", 0, 15)):
        v = np.asarray(d[k]).astype(np.float32)
        if not np.all((v >= lo) & (v <= hi) & (v == np.floor(v))): bad.append("range of " + k)
    if np.any(np.asarray(d["z0"]).astype(np.float32)[..., W - 1] != 0): bad.append("last column of z0")
    return bad
def reference(bills, due, z0, wt):
    e = bills.astype(np.int64).reshape(N, 8, 16, L); a = due.astype(np.float32).astype(np.int64).reshape(N, 8, 16, L)
    z = z0.astype(np.float32).astype(np.int64).reshape(N, 8, 16, W); w = wt.astype(np.float32).astype(np.int64).reshape(N, 8, 16, 1)
    lower = np.tri(L, k=-1).astype(bool)
    for rnd in range(RO):
        after = []; where_to = []
        for q in range(N):
            v = np.take_along_axis(z[q], e[q].reshape(8, 1, 16 * L), 2).reshape(8, 16, 16, L)
            covers = np.add.reduce((v >= a[q][:, :, None, :]).astype(np.int64), axis=1)
            k = np.max(np.where(covers >= H, ROW, -1), axis=1)
            has = k >= 0; x = np.take_along_axis(e[q], np.maximum(k, 0)[:, None, :], 1)[:, 0]
            x = np.where(has, x, W - 1)
            wait = has & np.any((x[:, :, None] == x[:, None, :]) & lower, axis=2); pays = has & ~wait
            new = np.maximum(np.take_along_axis(z[q], x[:, None, :], 2) - a[q], 0)
            for g in range(8):
                zg = z[q, g]; m = pays[g]; zg[:, x[g][m]] = new[g][:, m]
            c = np.add.reduce(w[q] * new, axis=1) & (W - 1)
            go = pays & (k > 0) & (k < 15); kk = k[:, None, :]
            longer = np.where(ROW <= kk, e[q], np.where(ROW == kk + 1, c[:, None, :], W - 1))
            after.append(np.where(go[:, None, :], longer, e[q]))
            where_to.append(np.where(wait, q, np.where(go, c & (N - 1), -1)))
        e2 = np.full((N, 8, 16, L), W - 1, np.int64); a2 = np.ones((N, 8, 16, L), np.int64)
        for q in range(N):
            for g in range(8):
                for d in range(N):
                    ln = np.flatnonzero(where_to[q][g] == d)[:C]; at = C * q; h = (g + (d != q)) % 8
                    e2[d, h][:, at:at + len(ln)] = after[q][g][:, ln]
                    a2[d, h][:, at:at + len(ln)] = a[q, g][:, ln]
        e, a = e2, a2
    return {"yz": z.reshape(N, 128, W).astype(np.float32).astype(BF), "ye": e.reshape(N, 128, L).astype(np.float32), "ya": a.reshape(N, 128, L).astype(np.float32).astype(BF)}

@@ -1,0 +1,521 @@
+from concourse.bass import DstId, RemoteDMATransfer
+from concourse.mybir import AluOpType as Op, ActivationFunctionType as Fn
+
+N, L, C, W, RO = 4, 384, 96, 2048, 5
+SROWS = [1, 5, 9, 13, 11, 15]
+MAGIC = 12582912.0
+BIG = 1048576.0
+f32, bf, f16, i32, u16 = "float32", "bfloat16", "float16", "int32", "uint16"
+
+
+def sb(n, d):
+    return ("sbuf", [128] + (n if isinstance(n, list) else [n]), d)
+
+
+SCRATCH = {"PHI": sb([12, 2, 16], f16), "CMP": sb([L, 16], bf), "NS": ("psum", [128, 16, 2, 16], f32)}
+for _d, _l in ((f32, "P NT S T1 T2 ab:24 gk:24 xs:24 ex:24 y:24 y2:24 DU:24 q1:24 YE col:8 K:392 U:24 m2:16 c0:96 lj:24 la:24 lb:24"),
+               (bf, "A Z:2432 wcol:16 AU VB:2496 d n lose kk:24 e:24 nq:24 ind:96 sc:96 EQ:9216 YA B8:8 WB:144 WW:144 WH:144 "
+                    "BD:128 BW:128 TM:128 IB:144 NB:144 I8:128 N8:128 SH:128 SW:1024 SEL:2048 LT:1920 ones rows:768 crow RM:96"),
+               (i32, "bil r:24 x:24 rk:24 ci:24 rel:24 ri:8 rj:8 lq:24"),
+               (f16, "xf:24 prod:96 XR CC:96 DO:24"),
+               (u16, "OFF xo:24 so:24 slot:24 LS:96")):
+    for _n in _l.split():
+        SCRATCH[_n.split(":")[0]] = sb(int(_n.split(":")[1]) if ":" in _n else L, _d)
+for _n in ("CP", "b1", "b2", "b3", "b5", "b6", "b7"):
+    SCRATCH[_n] = ("psum", [128, 512], f32)
+for _r in range(RO):
+    SCRATCH["W%d" % _r] = sb(5 * L, f32)
+    SCRATCH["LA%d" % _r] = sb(L, f32)
+SEMAPHORES = (["ev", "es", "et", "eg", "acc", "sent"] + ["l%d" % k for k in range(6)] + ["o%d" % k for k in range(8)]
+              + ["ar%d_%d" % (r, q) for r in range(RO) for q in range(N)])
+
+
+def rank_program(g, core, T, topo):
+    q = T.rank_of(core)
+    if q is None:
+        return
+    ops = []
+    Q = {"v": g.vector, "s": g.scalar, "t": g.tensor, "g": g, "y": g.sync}
+
+    def a(name, *idx):
+        where, shape, _ = SCRATCH[name]
+        rows = slice(None)
+        if idx and isinstance(idx[0], tuple):
+            rows = slice(*idx[0]); idx = idx[1:]
+        idx = list(idx) + [slice(None)] * (len(shape) - 1 - len(idx))
+        m, size = 1, 1
+        for k, n in reversed(list(zip(idx, shape[1:]))):
+            rg = range(n)[k] if isinstance(k, slice) else [k]
+            m = sum(m << (size * i) for i in rg); size *= n
+        if where == "psum":
+            m = 1
+        return {"ap": T[name][tuple([rows] + idx)], "reg": [(name, m)], "ps": where == "psum"}
+
+    def s(x, y=None, z=None):
+        return slice(x, y, z)
+
+    def ix(win, off):
+        return {"ap": win["ap"].indirect(off["ap"]), "reg": win["reg"], "off": off["reg"], "ps": False}
+
+    def ap(x):
+        return x["ap"] if isinstance(x, dict) else x
+
+    def op(eng, fn, out, ins, sem=None):
+        rd, wr = [], []
+        for x in ins:
+            if isinstance(x, dict):
+                rd += x["reg"] + x.get("off", [])
+                if x["ps"]:
+                    wr += [(n, m, "ps") for n, m in x["reg"]]
+        if isinstance(out, dict):
+            wr += out["reg"]; rd += out.get("off", [])
+        ops.append({"e": eng, "fn": fn, "rd": rd, "wr": wr, "sem": sem})
+
+    def tt(out, x, y, o):
+        op("v", lambda: g.vector.tensor_tensor(ap(out), ap(x), ap(y), o), out, [x, y])
+
+    def ts(out, x, s1, o0, s2=None, o1=None):
+        if o1 is None:
+            op("v", lambda: g.vector.tensor_scalar(ap(out), ap(x), ap(s1), None, o0), out, [x, s1])
+        else:
+            op("v", lambda: g.vector.tensor_scalar(ap(out), ap(x), ap(s1), ap(s2), o0, o1), out, [x, s1, s2])
+
+    def cp(out, x):
+        op("v", lambda: g.vector.tensor_copy(ap(out), ap(x)), out, [x])
+
+    def ms(out, v):
+        op("v", lambda: g.vector.memset(ap(out), v), out, [])
+
+    def scan(out, d0, d1, init, o0, o1):
+        op("v", lambda: g.vector.tensor_tensor_scan(ap(out), ap(d0), ap(d1), init, o0, o1), out, [d0, d1])
+
+    def act(out, x, f=Fn.Identity, bias=0.0, scale=1.0):
+        op("s", lambda: g.scalar.activation(ap(out), ap(x), f, bias=bias, scale=ap(scale)), out, [x, scale])
+
+    def mm(out, lhs, rhs, start, stop):
+        op("t", lambda: g.tensor.matmul(ap(out), ap(lhs), ap(rhs), start, stop), out, [lhs, rhs])
+
+    def iota(out, pat, base, cm, flt=True):
+        if flt:
+            op("g", lambda: g.iota(ap(out), pat, base, cm, allow_small_or_imprecise_dtypes=True), out, [])
+        else:
+            op("g", lambda: g.iota(ap(out), pat, base, cm), out, [])
+
+    def sel(out, x, pat, cmp_, fill, base, cm):
+        op("g", lambda: g.affine_select(ap(out), ap(x), pat, cmp_, fill, base, cm), out, [x])
+
+    def dma(eng, out, x, sem, **kw):
+        ins = [x, out] if kw else [x]
+        op(eng, lambda: Q[eng].dma_start(ap(out), ap(x), **kw), out, ins, sem)
+
+    scol = a("col", s(0, 1))
+    I = a("IB", s(15, 143))
+    one1 = lambda n: a("ones", (0, 1), s(0, n))
+    row = lambda k, n=128: a("rows", (0, 1), s(128 * k, 128 * k + n))
+    selk = lambda k: a("SEL", s(128 * k, 128 * k + 128))
+
+    def turn(k):
+        return k if 0 < k < N - 1 else 0
+
+    def place(k, src):
+        return (src - turn(k)) % N
+
+    nt = 6 * turn(q)
+    nh = 24 - nt
+    pieces = [(0, nt, nh)] + ([(nh, 0, nt)] if nt else [])
+    own = (6 * place(q, q), 6 * place(q, q) + 6)
+    far = (6, 24) if own[0] == 0 else (0, 18)
+    lists = {24: 0, 6: 24, 18: 30}
+
+    for i, (x, y, n) in enumerate(pieces):
+        dma("y", a("bil", s(16 * x, 16 * (x + n))), T.bills[:, 16 * y:16 * (y + n)], "l%d" % i)
+        dma("s", a("A", s(16 * x, 16 * (x + n))), T.due[:, 16 * y:16 * (y + n)], "l%d" % (2 + i))
+    dma("y", a("Z", s(0, W)), T.z0[:], "l4")
+    op("s", lambda: g.scalar.dma_start(T.wcol[:, 0:1], T.wt[:]), a("wcol"), [], "l5")
+
+    def swap(sh):
+        for h in range(2):
+            for h2 in range(2):
+                m = a("SW", s(512 * sh + 256 * h + 128 * h2, 512 * sh + 256 * h + 128 * h2 + 128))
+                base = 16 * sh - 16 * h2 - 1000 * h
+                sel(m, m, [[-32, 4], [1000, 2], [-1, 16]], Op.is_equal, 0.0, base, 1)
+                if sh and not h2:
+                    sel(m, m, [[-32, 4], [1000, 2], [-1, 16]], Op.not_equal, 8192.0, base - 128, 1)
+
+    def make_list(nu):
+        c = s(0, nu)
+        ts(a("lq", c), a("lj", c), -(nu - 1) / 2.0, Op.add, 1.0 / nu, Op.mult)
+        ts(a("la", c), a("lq", c), 1.0 - 16.0 * nu, Op.mult)
+        tt(a("la", c), a("la", c), a("lb", c), Op.add)
+        cp(a("LS", s(lists[nu], lists[nu] + nu)), a("la", c))
+
+    def fills():
+        for name, x, y, v in (("BD", 0, 128, 1.0), ("SEL", 0, 2048, 256.0), ("SH", 0, 128, 1.0), ("SW", 512, 1024, 8192.0)):
+            for k in range(x, y, L):
+                act(a(name, s(k, min(y, k + L))), a("ones", s(0, min(y - k, L))), scale=v)
+
+    iota(a("ri"), [[0, 8]], 0, 1, False)
+    iota(a("U"), [[16, 24]], 0, 0)
+    ms(a("SW", s(0, 512)), 8192.0)
+    ms(a("ones"), 1.0)
+    swap(0)
+    ts(a("rj"), a("ri"), 15, Op.bitwise_and)
+    ms(a("WB"), 0.0)
+    cp(scol, a("rj", s(0, 1)))
+    ms(a("B8"), BIG)
+    ts(a("lj"), a("U"), scol, Op.add)
+    ms(a("IB"), 1.0)
+    ts(a("lb"), a("lj"), 16.0, Op.mult)
+    make_list(24)
+    for x, st in ((0, 2), (3, 16), (7, 16)):
+        ms(a("crow", s(x, L, st)), -8 * BIG)
+    for x, st in ((1, 4), (11, 16), (15, 16)):
+        ms(a("crow", s(x, L, st)), 0.0)
+    sel(a("IB"), a("IB"), [[-1, 144]], Op.is_equal, 0.0, 15, 1)
+    sel(a("B8"), a("B8"), [[-16, 8]], Op.is_ge, 0.0, 0, 1)
+    sel(a("WB", s(15, 143, 16)), a("B8"), [[16, 8]], Op.is_ge, 0.0, 15, -1)
+    fills()
+    act(a("NB"), a("IB"), scale=-1.0)
+    iota(a("K"), [[2048, 392]], 2047, 0)
+
+    def late_constants():
+        sel(a("BD"), a("BD"), [[-16, 8], [0, 16]], Op.is_ge, 0.0, 0, 1)
+        sel(a("BD"), a("BD"), [[16, 8], [0, 16]], Op.is_ge, 0.0, 15, -1)
+        sel(a("TM"), a("BD"), [[-1, 128]], Op.is_gt, 0.0, 0, 1)
+        iota(row(1), [[0, 8], [1, 16]], 0, 0)
+        iota(row(2), [[0, 8], [-256, 16]], 0, 0)
+        sel(a("SEL"), a("SEL"), [[-1, 16], [-16, 8], [0, 16]], Op.is_equal, 0.0, 0, 1)
+        iota(a("c0"), [[L, 4], [-16, 24]], -4 * L - 1, 0)
+
+    def last_constants():
+        sel(a("SH"), a("SH"), [[-1, 128]], Op.is_equal, 0.0, 16, 1)
+        sel(a("SH"), a("SH"), [[-1, 128]], Op.not_equal, 1.0, -112, 1)
+        swap(1)
+
+    def small_constants():
+        ms(a("RM"), 1.0)
+        ms(row(0), 0.0); ms(a("rows", (0, 2), s(128, 256)), 1.0 / 8192); ms(row(4), -23.0); ms(row(5), 44.5)
+        ts(a("m2"), a("U", s(0, 16)), 1.0 / 16, Op.mult, scol, Op.is_gt)
+        ts(a("DU"), a("lj"), float(W), Op.add, 1.0 / 512, Op.mult)
+
+    def scalar_constants():
+        act(a("I8"), I, scale=8192.0)
+        act(a("WH"), a("WB"), scale=0.5 / BIG)
+        act(a("TM"), a("TM"), scale=-1.0)
+        act(a("N8"), I, scale=-8192.0)
+        for k in range(1, 16):
+            act(a("LT", s(128 * k - 128, 128 * k)), a("BD"), scale=a("m2", s(k, k + 1)))
+
+    def round_constants():
+        w = a("wcol", s(0, 1))
+        return [[lambda: ts(a("WW"), a("WB"), w, Op.mult, 1.0 / BIG, Op.mult),
+                 lambda: ts(a("BW"), a("BD"), w, Op.mult, 1.0 / 8192, Op.mult)],
+                [lambda: ts(a("RM", s(0, 96, 24)), a("RM", s(0, 96, 24)), 0.0, Op.mult),
+                 lambda: ts(a("CC"), a("c0"), scol, Op.subtract),
+                 lambda: ts(a("DO"), a("lj"), 4.0 * L, Op.add)],
+                [lambda: ms(a("crow", s(16 * own[0] + 3, 16 * own[1], 4)), 0.0), lambda: make_list(6)],
+                [lambda: make_list(18)]]
+
+    def unpack(src, seg, sh):
+        u0, u1 = seg
+        au = a("AU" if sh else "A", s(16 * u0, 16 * u1))
+        ts(au, src, MAGIC, Op.add, -MAGIC, Op.add)
+        tt(a("PHI", s(u0 // 2, u1 // 2)), src, au, Op.subtract)
+
+    def names_pe(seg, sh):
+        u0, u1 = seg
+        b, c = s(u0 // 2, u1 // 2), s(16 * u0, 16 * u1)
+        for h2 in range(2):
+            for h in range(2):
+                k = 512 * sh + 256 * h + 128 * h2
+                mm(a("NS", b, h2), a("SW", s(k, k + 128)), a("PHI", b, h), h == 0, h == 1)
+        if sh:
+            mm(a("b6", c), a("SH"), a("AU", c), True, False)
+            mm(a("b6", c), a("SH"), a("PHI", b), False, True)
+            mm(a("b7", c), a("SH"), a("AU", c), True, True)
+            act(a("P", c), a("b6", c))
+            act(a("A", c), a("b7", c))
+
+    def names_v(seg):
+        u0, u1 = seg
+        b, c, nu = s(u0 // 2, u1 // 2), s(16 * u0, 16 * u1), u1 - u0
+        op("v", lambda: g.vector.transpose(ap(a("NT", c)), ap(a("NS", b))), a("NT", c), [a("NS", b)])
+        ts(a("OFF", c), ix(a("NT", c), a("LS", s(lists[nu], lists[nu] + nu))), 2047.0, Op.add)
+
+    bank = [0]
+
+    def compare(seg):
+        u0, u1 = seg
+        nu, c, z = u1 - u0, s(16 * u0, 16 * u1), a("Z", s(0, W))
+        w = 16 * nu
+        off = lambda p: a("OFF", s(16 * u0 + nu * p, 16 * u0 + nu * (p + 1)))
+        at0 = lambda p: 1728 + w * (p // 2) if nu == 6 else w * SROWS.index(p)
+        vb = lambda p: a("VB", s(at0(p), at0(p) + w))
+        at = {}
+
+        def V(*ps):
+            for p in ps:
+                tt(a("CMP", c, p), ix(z, off(p)), a("P", c), Op.is_ge)
+
+        def G(*ps):
+            for p in ps:
+                act(vb(p), ix(z, off(p)))
+
+        def D(*ps):
+            nm = "b%d" % (1 + bank[0] % 3); bank[0] += 1
+            for i, p in enumerate(ps):
+                at[p] = a(nm, s(w * i, w * i + w))
+                mm(at[p], I, vb(p), True, False)
+                mm(at[p], a("NB", s(15, 143)), a("A", c), False, True)
+
+        def S(*ps):
+            for p in ps:
+                act(a("CMP", c, p), at[p], Fn.Sign, bias=0.25)
+
+        def Cn(p0, st, stop=False, x=u0, y=u1):
+            for k in range(16):
+                mm(a("CP", s(16 * x + p0, 16 * y, st)), a("WB", s(15 - k, 143 - k)),
+                   a("CMP", s(16 * x + k, 16 * y, 16), s(p0, 16, st)), False, stop and k == 15)
+
+        return V, G, D, S, Cn
+
+    def compare_many(seg):
+        V, G, D, S, Cn = compare(seg)
+        G(1); D(1); G(5); D(5); S(1); G(9); D(9); S(5); V(0, 4, 8, 12); G(13); Cn(0, 4, False, 0, 24); D(13); S(9)
+        G(11); D(11); S(13); G(15); Cn(1, 4); D(15); V(2, 6, 10, 14); Cn(2, 4); S(11, 15); V(3, 7); Cn(3, 4, True)
+
+    def open_counts():
+        mm(a("CP", s(0, L)), one1(128), a("crow", (0, 1)), True, False)
+
+    def add_places():
+        dma("g", a("NT"), a("K", s(1, L + 1)), "acc", accum_op=Op.add)
+
+    def arrived(r):
+        for src in range(N):
+            if src != q:
+                x = C * place(q, src)
+                ops.append({"e": "x", "rd": [], "wr": a("LA%d" % r, s(x, x + C))["reg"], "sem": "ar%d_%d" % (r, src),
+                            "n": len(plan(src)[q])})
+
+    def plan(r0):
+        c0 = T.cores[r0]
+        others = [k for k in range(N) if k != r0]
+        few = min((topo.engines(c0, T.cores[k]) for k in others), key=len)
+        out = [k for k in others if topo.engines(c0, T.cores[k]) == few]
+        res = {}
+        for i, k in enumerate(out):
+            m = len(few) // len(out)
+            res[k] = few[m * i:m * i + m]
+        for k in others:
+            if k not in out:
+                res[k] = [e for e in topo.engines(c0, T.cores[k]) if e not in few]
+        return res
+
+    sent = [0]
+
+    def send(r):
+        pl = plan(q)
+        trs, rd = [], []
+        for j in range(N - 1):
+            k = (q + 1 + j) % N
+            rid, pid = topo.addr(T.cores[k], core)
+            src = a("W%d" % r, s(L * j, L * j + C)); rd.append(src)
+            x = C * place(k, q)
+            trs.append(RemoteDMATransfer(dst_ids=[DstId(rid=rid, pnc=pid)], dma_engine_mask=sum(1 << e for e in pl[k]),
+                                         remote_sem=T.sem["ar%d_%d" % (r, q)], src=ap(src), dst=T["LA%d" % r][:, x:x + C]))
+            sent[0] += len(pl[k])
+        op("g", lambda: g.remote_dma_fused(trs, local_sem=T.sem.sent), None, rd, "none")
+
+    def settle(r):
+        full, t24, t96 = s(0, L), s(0, 24), s(0, 96)
+        extra = round_constants() if r == 0 else [[], [], [], []]
+
+        def more(k):
+            for f in extra[k]:
+                f()
+
+        for j in range(N):
+            iota(a("W%d" % r, s(L * j, L * j + C)), [[0, C]], 1, 0)
+        if r == 0:
+            scalar_constants()
+            last_constants()
+        mm(a("b7", t24), row(4), row(5, 24), True, False)
+        mm(a("b5", full), row(0), one1(L), True, False)
+        mm(a("b1", full), row(2), one1(L), True, False)
+        mm(a("b2", full), a("rows", (0, 2), s(128, 256)), a("ones", (0, 2)), True, False)
+        mm(a("b2", full), I, a("A"), False, False)
+        scan(a("S"), a("CP", full), a("NT"), 0.0, Op.max, Op.min)
+        tt(a("r"), a("S", s(15, L, 16)), a("K", s(0, L, 16)), Op.max)
+        ts(a("x"), a("r"), W - 1, Op.bitwise_and)
+        ts(a("rk"), a("r"), 11, Op.arith_shift_right)
+        cp(a("xf"), a("x"))
+        cp(a("xo"), a("x"))
+        for k in range(16):
+            mm(a("b3", s(k, L, 16)), selk(k), a("xf"), True, True)
+        ts(a("xs"), a("x"), 1.0 / 512, Op.mult)
+        tt(a("kk"), a("rk"), a("U"), Op.subtract)
+        tt(a("d"), ix(a("Z", s(0, W)), a("xo")), a("A"), Op.subtract)
+        for x, y, n in pieces:
+            ts(a("XR", s(16 * y, 16 * (y + n))), a("b3", s(16 * x, 16 * (x + n))), 1.0 / (256 * 512), Op.mult)
+        more(0)
+        act(a("n"), a("d"), Fn.Relu)
+        act(a("ab"), a("kk"), Fn.Abs, bias=-68.0, scale=8.0)
+        act(a("gk"), a("ab"), bias=58.0, scale=-1.0)
+        mm(a("b7", t24), a("I8"), a("kk"), False, False)
+        for k in range(16):
+            mm(a("b1", s(k, L, 16)), selk(k), a("kk"), False, False)
+        mm(a("b2", full), a("BW"), a("n"), False, False)
+        for lane in range(24):
+            u = (lane - nt) % 24
+            ts(a("EQ", s(400 * lane, L * (lane + 1))), a("XR", s(16 * lane, L)), a("xs", s(u, u + 1)), Op.is_equal)
+            if lane < 23:
+                mm(a("b5", s(16 * lane + 16, L)), a("BD"), a("EQ", s(400 * lane + 16, L * (lane + 1))), False, False)
+            if lane == 2:
+                for k in range(16):
+                    mm(a("b7", t24), a("WW", s(15 - k, 143 - k)), a("n", s(k, L, 16)), False, k == 15)
+                act(a("q1"), a("b7", t24), bias=MAGIC, scale=1.0 / 2048)
+                act(a("nq"), a("q1"), bias=(MAGIC - 1) / 1024, scale=-1.0 / 1024)
+        for k in range(1, 16):
+            mm(a("b5", s(k, L, 16)), a("LT", s(128 * k - 128, 128 * k)), a("EQ", s(k, 24 * L, 400)), False, k == 15)
+        ts(a("ci"), a("b7", t24), 1023.5 + 3 - q, Op.add)
+        more(1)
+        ts(a("rel"), a("ci"), N - 1, Op.bitwise_and)
+        tt(a("e"), a("rel"), a("gk"), Op.min)
+        tt(a("ex"), a("e"), a("xs"), Op.subtract)
+        ts(a("lose"), a("b5", full), 0.5, Op.is_gt)
+        more(2)
+        for k in range(16):
+            mm(a("b2", s(k, L, 16)), selk(k), a("nq"), False, False)
+        mm(a("b6", t24), row(0), one1(24), True, False)
+        for x, y, n in pieces:
+            mm(a("b6", s(y, y + n)), I, a("e", s(x, x + n)), False, False)
+        for k in range(16):
+            mm(a("b6", t24), a("WH", s(15 - k, 143 - k)), a("lose", s(k, L, 16)), False, k == 15)
+        for nm, m in (("b1", "I8"), ("b2", "N8")):
+            for x, y, n in pieces:
+                mm(a(nm, s(16 * x, 16 * (x + n))), a(m), a("lose", s(16 * y, 16 * (y + n))), False, x + n == 24)
+        for j in range(N):
+            ts(a("ind", s(24 * j, 24 * j + 24)), a("b6", t24), float(j), Op.is_equal if j < N - 1 else Op.is_ge)
+        for x, y, n in pieces:
+            tt(a("y", s(x, x + n)), a("b6", s(y, y + n)), a("ex", s(x, x + n)), Op.subtract)
+        scan(a("sc"), a("RM"), a("ind"), 0.0, Op.mult, Op.add)
+        mm(a("b5", t96), I, a("CC"), True, False)
+        mm(a("b5", t96), a("TM"), a("ind"), False, False)
+        mm(a("b5", t96), a("BD"), a("sc"), False, True)
+        tt(a("T1"), a("P"), a("b1", full), Op.min)
+        tt(a("prod"), a("ind"), a("b5", t96), Op.mult)
+        for x, y, n in pieces:
+            mm(a("b7", s(x, x + n)), I, a("DO", s(y, y + n)), True, False)
+            for j in range(N):
+                mm(a("b7", s(x, x + n)), I, a("prod", s(24 * j + y, 24 * j + y + n)), False, j == N - 1)
+        tt(a("T2"), a("A"), a("b2", full), Op.min)
+        cp(a("slot"), a("b7", t24))
+        tt(a("y2"), a("y"), a("DU"), Op.min)
+        tt(ix(a("W%d" % r), a("slot")), a("T1"), a("T2"), Op.max)
+        ts(a("so"), a("y2"), 512.0, Op.mult)
+        send(r)
+        return extra[3]
+
+    def pay():
+        cp(ix(a("Z"), a("so")), a("n"))
+
+    small_constants()
+    ts(a("PHI"), a("bil"), -2047.0, Op.add, 1.0 / 8192, Op.mult)
+    names_pe((0, 24), 0)
+    mm(a("b6", s(0, L)), I, a("A"), True, False)
+    mm(a("b6", s(0, L)), I, a("PHI"), False, True)
+    act(a("P"), a("b6", s(0, L)))
+    names_v((0, 24))
+    add_places()
+    late_constants()
+    open_counts()
+    compare_many((0, 24))
+    left = settle(0)
+    oc, fc = s(16 * own[0], 16 * own[1]), s(16 * far[0], 16 * far[1])
+    for r in range(1, RO):
+        mine = a("W%d" % (r - 1), s(3 * L, 3 * L + C))
+        act(a("P", oc), mine)
+        unpack(mine, own, 0)
+        names_pe(own, 0)
+        open_counts()
+        pay()
+        names_v(own)
+        for f in left:
+            f()
+        V, G, D, S, Cn = compare(own)
+        G(1, 3, 5, 7); D(1, 3, 5, 7); G(9, 11, 13, 15); D(9, 11, 13, 15); S(1, 3, 5, 7); S(9, 11, 13, 15)
+        V(2, 6, 10, 14)
+        arrived(r - 1)
+        unpack(a("LA%d" % (r - 1), fc), far, 1)
+        names_pe(far, 1)
+        V(0, 4, 8, 12)
+        Cn(2, 4)
+        Cn(1, 2)
+        names_v(far)
+        add_places()
+        compare_many(far)
+        left = settle(r)
+    pay()
+    for i in range(2):
+        dma("ys"[i], T.yz[:, 1024 * i:1024 * i + 1024], a("Z", s(1024 * i, 1024 * i + 1024)), "o%d" % i)
+    mine = a("W%d" % (RO - 1), s(3 * L, 3 * L + C))
+    unpack(mine, own, 0)
+    cp(a("YA", oc), a("A", oc))
+    ts(a("YE", oc), a("PHI", s(own[0] // 2, own[1] // 2)), 8192.0, Op.mult, 2047.0, Op.add)
+    arrived(RO - 1)
+    unpack(a("LA%d" % (RO - 1), fc), far, 1)
+    mm(a("b7", fc), a("SH"), a("AU", fc), True, True)
+    mm(a("b6", fc), a("SH"), a("PHI", s(far[0] // 2, far[1] // 2)), True, True)
+    act(a("YA", fc), a("b7", fc))
+    ts(a("YE", fc), a("b6", fc), 8192.0, Op.mult, 2047.0, Op.add)
+    for i, (x, y, n) in enumerate(pieces):
+        dma("s", T.ya[:, 16 * y:16 * (y + n)], a("YA", s(16 * x, 16 * (x + n))), "o%d" % (4 + i))
+        dma("y", T.ye[:, 16 * y:16 * (y + n)], a("YE", s(16 * x, 16 * (x + n))), "o%d" % (6 + i))
+
+    def meet(xs, ys):
+        return any(x[0] == y[0] and x[1] & y[1] for x in xs for y in ys)
+
+    by = {}
+    for i, o in enumerate(ops):
+        o["dep"] = {}
+        cand = set()
+        for x in o["rd"] + o["wr"]:
+            cand.update(by.get(x[0], []))
+        for j in cand:
+            p = ops[j]
+            real = [x for x in p["wr"] if len(x) == 2]
+            same = p["e"] == o["e"] and p["sem"] is None and o["sem"] is None
+            if same:
+                hit = o["e"] != "t" and (meet(o["rd"] + o["wr"], real) or meet([x for x in o["wr"] if len(x) == 2], p["rd"]))
+            else:
+                hit = meet(o["rd"], real) or meet(o["wr"], p["rd"] + p["wr"])
+            if hit and p["sem"] != "none" and o["e"] != "x":
+                key = p["sem"] or "e" + p["e"]
+                o["dep"][key] = max(o["dep"].get(key, -1), j)
+        for x in set(x[0] for x in o["rd"] + o["wr"]):
+            by.setdefault(x, []).append(i)
+    seen = {e: {} for e in Q}
+    for o in ops:
+        if o["e"] != "x":
+            o["dep"] = {k: j for k, j in o["dep"].items() if j > seen[o["e"]].get(k, -1)}
+            seen[o["e"]].update(o["dep"])
+            for j in o["dep"].values():
+                ops[j]["sig"] = True
+    count = {}
+    for o in ops:
+        key = o["sem"] or "e" + o["e"]
+        if o["e"] == "x":
+            count[key] = o["at"] = o["n"]
+            continue
+        for k, j in o["dep"].items():
+            Q[o["e"]].wait_ge(T.sem[k], ops[j]["at"])
+        ins = o["fn"]()
+        if key == "none":
+            continue
+        if o["sem"] or o.get("sig"):
+            n = 16 if o["sem"] else 1
+            ins.then_inc(T.sem[key], n)
+            count[key] = o["at"] = count.get(key, 0) + n
+    count["sent"] = sent[0]
+    for k, n in count.items():
+        g.wait_ge(T.sem[k], n)

@@ -1,32 +1,38 @@
 from concourse.bass import DstId, RemoteDMATransfer
-from concourse.mybir import AluOpType as Op, ActivationFunctionType as Fn
+from concourse.mybir import AluOpType as Op, ActivationFunctionType as Fn, AxisListType as Ax
 
 N, L, C, W, RO = 4, 384, 96, 2048, 5
-SROWS = [1, 5, 9, 13, 11, 15]
 MAGIC = 12582912.0
 BIG = 1048576.0
 f32, bf, f16, i32, u16 = "float32", "bfloat16", "float16", "int32", "uint16"
+CYCLE = 0.83
+CFG = {"issue": 100, "pe": 0.45, "gather": 1.56, "scatter": 3.8, "fix": 20, "hop": 180, "dma": 2000, "near_ns": 2600, "far_ns": 3600,
+       "patience": {"v": 1.2, "s": 0, "t": 0}, "first": 6, "own": 10, "near": 7, "far": 6,
+       "start": "Sacd Sade Saef Saab Safg Sabc Va048 Ca04 Va159 Ca14 Va26 Ca24 Va37 Ca34",
+       "later": "Socg So8c So68 Vo012345 Sncg Sn9c Vn012345678 Sfce Sfeg Sfab Sfbc Co01 Cn01 Vf048 Cf04 Vf159 Cf14 Vf26 Cf24 Vf37 Cf34"}
 
 
 def sb(n, d):
     return ("sbuf", [128] + (n if isinstance(n, list) else [n]), d)
 
 
-SCRATCH = {"PHI": sb([12, 2, 16], f16), "CMP": sb([L, 16], bf), "NS": ("psum", [128, 16, 2, 16], f32)}
-for _d, _l in ((f32, "P NT S T1 T2 ab:24 gk:24 xs:24 ex:24 y:24 y2:24 DU:24 q1:24 YE col:8 K:392 U:24 m2:16 c0:96 lj:24 la:24 lb:24"),
-               (bf, "A Z:2432 wcol:16 AU VB:2496 d n lose kk:24 e:24 nq:24 ind:96 sc:96 EQ:9216 YA B8:8 WB:144 WW:144 WH:144 "
-                    "BD:128 BW:128 TM:128 IB:144 NB:144 I8:128 N8:128 SH:128 SW:1024 SEL:2048 LT:1920 ones rows:768 crow RM:96"),
-               (i32, "bil r:24 x:24 rk:24 ci:24 rel:24 ri:8 rj:8 lq:24"),
-               (f16, "xf:24 prod:96 XR CC:96 DO:24"),
+SCRATCH = {"PHI": sb([12, 2, 16], f16), "CMP": sb([L, 16], bf), "NS": ("psum", [128, 16, 2, 16], f32),
+           "CP": ("psum", [128, 512], f32), "EQ": sb([24, L], bf), "crow0": sb([24, 16], bf), "crow1": sb([24, 16], bf)}
+for _d, _l in ((f32, "P NT NK S T1 T2 ab:24 gk:24 xs:24 ex:24 y:24 y2:24 DU:24 q1:24 YE col:8 K:392 U:24 c0:96 lj:24 lb:24 "
+                     "la:48 ID:2048 h16:16 w16:16 v16:16 m16:16 wj:8"),
+               (bf, "A Z:2432 wcol:16 AU VB:6144 d n lose kk:24 e:24 nq:24 ind:96 sc:96 B8:8 WB:144 WW:144 WH:144 U16 M16 "
+                    "BD:128 BW:128 BJ:128 TM:128 IB:144 NB:144 I8:128 N8:128 SH:128 SW:1024 SEL:2048 ones rows:768 RM:96"),
+               (i32, "bil r:24 x:24 rk:24 ci:24 rel:24 ri:8 rj:8 lq:48"),
+               (f16, "prod:96 XR CC:96 DO:24"),
                (u16, "OFF xo:24 so:24 slot:24 LS:96")):
     for _n in _l.split():
         SCRATCH[_n.split(":")[0]] = sb(int(_n.split(":")[1]) if ":" in _n else L, _d)
-for _n in ("CP", "b1", "b2", "b3", "b5", "b6", "b7"):
+for _n in ("b1", "b2", "b3", "b5", "b6", "b7"):
     SCRATCH[_n] = ("psum", [128, 512], f32)
 for _r in range(RO):
     SCRATCH["W%d" % _r] = sb(5 * L, f32)
     SCRATCH["LA%d" % _r] = sb(L, f32)
-SEMAPHORES = (["ev", "es", "et", "eg", "acc", "sent"] + ["l%d" % k for k in range(6)] + ["o%d" % k for k in range(8)]
+SEMAPHORES = (["ev", "es", "et", "eg", "acc0", "acc1", "keys", "sent", "out"] + ["l%d" % k for k in range(4)]
               + ["ar%d_%d" % (r, q) for r in range(RO) for q in range(N)])
 
 
@@ -34,11 +40,11 @@ def rank_program(g, core, T, topo):
     q = T.rank_of(core)
     if q is None:
         return
-    ops = []
+    ops, aside = [], [False]
     Q = {"v": g.vector, "s": g.scalar, "t": g.tensor, "g": g, "y": g.sync}
 
     def a(name, *idx):
-        where, shape, _ = SCRATCH[name]
+        where, shape, kind = SCRATCH[name]
         rows = slice(None)
         if idx and isinstance(idx[0], tuple):
             rows = slice(*idx[0]); idx = idx[1:]
@@ -47,20 +53,32 @@ def rank_program(g, core, T, topo):
         for k, n in reversed(list(zip(idx, shape[1:]))):
             rg = range(n)[k] if isinstance(k, slice) else [k]
             m = sum(m << (size * i) for i in rg); size *= n
-        if where == "psum":
-            m = 1
-        return {"ap": T[name][tuple([rows] + idx)], "reg": [(name, m)], "ps": where == "psum"}
+        return {"ap": T[name][tuple([rows] + idx)], "reg": [(name, 1 if where == "psum" else m)], "ps": where == "psum",
+                "n": m.bit_count(), "two": kind in (bf, f16, u16)}
 
     def s(x, y=None, z=None):
         return slice(x, y, z)
 
     def ix(win, off):
-        return {"ap": win["ap"].indirect(off["ap"]), "reg": win["reg"], "off": off["reg"], "ps": False}
+        return {"ap": win["ap"].indirect(off["ap"]), "reg": win["reg"], "off": off["reg"], "ps": False, "n": 16 * off["n"]}
 
     def ap(x):
         return x["ap"] if isinstance(x, dict) else x
 
-    def op(eng, fn, out, ins, sem=None):
+    def span(eng, out, ins, sem, both):
+        if sem:
+            return CFG["issue"]
+        n, x = out["n"], (ins or [out])[0]
+        if eng == "t":
+            return max(64, n) * CFG["pe"]
+        if eng == "g":
+            return 150 + 2 * n * CYCLE
+        if "off" in out or "off" in x:
+            return 60 + n * CYCLE * CFG["scatter" if "off" in out else "gather"]
+        per = 1 if eng == "s" else (1 if x["ps"] or ins[1]["ps"] else 2) if both else 0.5 if out["two"] and x["two"] else 1
+        return CFG["fix"] + max(64, n * per) * CYCLE
+
+    def op(eng, fn, out, ins, sem=None, both=False):
         rd, wr = [], []
         for x in ins:
             if isinstance(x, dict):
@@ -69,10 +87,10 @@ def rank_program(g, core, T, topo):
                     wr += [(n, m, "ps") for n, m in x["reg"]]
         if isinstance(out, dict):
             wr += out["reg"]; rd += out.get("off", [])
-        ops.append({"e": eng, "fn": fn, "rd": rd, "wr": wr, "sem": sem})
+        ops.append({"e": eng, "fn": fn, "rd": rd, "wr": wr, "sem": sem, "ns": span(eng, out, ins, sem, both), "aside": aside[0]})
 
     def tt(out, x, y, o):
-        op("v", lambda: g.vector.tensor_tensor(ap(out), ap(x), ap(y), o), out, [x, y])
+        op("v", lambda: g.vector.tensor_tensor(ap(out), ap(x), ap(y), o), out, [x, y], both=True)
 
     def ts(out, x, s1, o0, s2=None, o1=None):
         if o1 is None:
@@ -108,32 +126,42 @@ def rank_program(g, core, T, topo):
         ins = [x, out] if kw else [x]
         op(eng, lambda: Q[eng].dma_start(ap(out), ap(x), **kw), out, ins, sem)
 
-    scol = a("col", s(0, 1))
-    I = a("IB", s(15, 143))
+    scol, wcol = a("col", s(0, 1)), a("wcol", s(0, 1))
+    I, NI = a("IB", s(15, 143)), a("NB", s(15, 143))
     one1 = lambda n: a("ones", (0, 1), s(0, n))
     row = lambda k, n=128: a("rows", (0, 1), s(128 * k, 128 * k + n))
     selk = lambda k: a("SEL", s(128 * k, 128 * k + 128))
+    full, t24, t96, z = s(0, L), s(0, 24), s(0, 96), a("Z", s(0, W))
 
-    def turn(k):
-        return k if 0 < k < N - 1 else 0
+    near_r = [k for k in range(N) if k != q and T.cores[k] in topo.cores_of(core)]
+    far_r = [k for k in range(N) if k != q and k not in near_r]
+    own, near, far = [(6 * min(k), 6 * max(k) + 6) for k in ([q], near_r, far_r)]
+    every, home = (0, 24), (min(own[0], near[0]), max(own[1], near[1]))
+    cols = lambda seg: s(16 * seg[0], 16 * seg[1])
+    lists = {24: 0, 6: 24, 12: 30}
 
-    def place(k, src):
-        return (src - turn(k)) % N
-
-    nt = 6 * turn(q)
-    nh = 24 - nt
-    pieces = [(0, nt, nh)] + ([(nh, 0, nt)] if nt else [])
-    own = (6 * place(q, q), 6 * place(q, q) + 6)
-    far = (6, 24) if own[0] == 0 else (0, 18)
-    lists = {24: 0, 6: 24, 18: 30}
-
-    for i, (x, y, n) in enumerate(pieces):
-        dma("y", a("bil", s(16 * x, 16 * (x + n))), T.bills[:, 16 * y:16 * (y + n)], "l%d" % i)
-        dma("s", a("A", s(16 * x, 16 * (x + n))), T.due[:, 16 * y:16 * (y + n)], "l%d" % (2 + i))
-    dma("y", a("Z", s(0, W)), T.z0[:], "l4")
-    op("s", lambda: g.scalar.dma_start(T.wcol[:, 0:1], T.wt[:]), a("wcol"), [], "l5")
-
-    def swap(sh):
+    dma("y", a("bil"), T.bills[:], "l0")
+    dma("s", a("A"), T.due[:], "l1")
+    dma("y", z, T.z0[:], "l2")
+    op("s", lambda: g.scalar.dma_start(T.wcol[:, 0:1], T.wt[:]), a("wcol"), [], "l3")
+    aside[0] = True
+    iota(a("ri"), [[0, 8]], 0, 1, False)
+    iota(a("U"), [[16, 24]], 0, 0)
+    iota(a("U16"), [[0, 24], [1, 16]], 0, 0)
+    iota(a("K"), [[2048, 392]], 2047, 0)
+    for k in range(0, W, 512):
+        iota(a("ID", s(k, k + 512)), [[1, 512]], k, 0)
+    iota(a("c0"), [[L, 4], [-16, 24]], -4 * L - 1, 0)
+    for name, v in (("ones", 1.0), ("IB", 1.0), ("B8", BIG), ("WB", 0.0), ("h16", 0.5), ("RM", 1.0)):
+        ms(a(name), v)
+    ms(a("SW", s(0, 512)), 8192.0)
+    ms(a("RM", s(0, 96, 24)), 0.0)
+    ms(a("rows", (0, 2), s(128, 256)), 1.0 / 8192); ms(row(4), -23.0); ms(row(5), 44.5)
+    iota(row(1), [[0, 8], [1, 16]], 0, 0)
+    iota(row(2), [[0, 8], [-256, 16]], 0, 0)
+    for name, x, y, v in (("BD", 0, 128, 1.0), ("SH", 0, 128, 1.0), ("SW", 512, 768, 8192.0), ("SW", 768, 1024, 8192.0)):
+        act(a(name, s(x, y)), a("ones", s(0, y - x)), scale=v)
+    for sh in range(2):
         for h in range(2):
             for h2 in range(2):
                 m = a("SW", s(512 * sh + 256 * h + 128 * h2, 512 * sh + 256 * h + 128 * h2 + 128))
@@ -141,161 +169,111 @@ def rank_program(g, core, T, topo):
                 sel(m, m, [[-32, 4], [1000, 2], [-1, 16]], Op.is_equal, 0.0, base, 1)
                 if sh and not h2:
                     sel(m, m, [[-32, 4], [1000, 2], [-1, 16]], Op.not_equal, 8192.0, base - 128, 1)
-
-    def make_list(nu):
-        c = s(0, nu)
-        ts(a("lq", c), a("lj", c), -(nu - 1) / 2.0, Op.add, 1.0 / nu, Op.mult)
-        ts(a("la", c), a("lq", c), 1.0 - 16.0 * nu, Op.mult)
-        tt(a("la", c), a("la", c), a("lb", c), Op.add)
-        cp(a("LS", s(lists[nu], lists[nu] + nu)), a("la", c))
-
-    def fills():
-        for name, x, y, v in (("BD", 0, 128, 1.0), ("SEL", 0, 2048, 256.0), ("SH", 0, 128, 1.0), ("SW", 512, 1024, 8192.0)):
-            for k in range(x, y, L):
-                act(a(name, s(k, min(y, k + L))), a("ones", s(0, min(y - k, L))), scale=v)
-
-    iota(a("ri"), [[0, 8]], 0, 1, False)
-    iota(a("U"), [[16, 24]], 0, 0)
-    ms(a("SW", s(0, 512)), 8192.0)
-    ms(a("ones"), 1.0)
-    swap(0)
-    ts(a("rj"), a("ri"), 15, Op.bitwise_and)
-    ms(a("WB"), 0.0)
-    cp(scol, a("rj", s(0, 1)))
-    ms(a("B8"), BIG)
-    ts(a("lj"), a("U"), scol, Op.add)
-    ms(a("IB"), 1.0)
-    ts(a("lb"), a("lj"), 16.0, Op.mult)
-    make_list(24)
-    for x, st in ((0, 2), (3, 16), (7, 16)):
-        ms(a("crow", s(x, L, st)), -8 * BIG)
-    for x, st in ((1, 4), (11, 16), (15, 16)):
-        ms(a("crow", s(x, L, st)), 0.0)
+    sel(a("SH"), a("SH"), [[-1, 128]], Op.is_equal, 0.0, 16, 1)
+    sel(a("SH"), a("SH"), [[-1, 128]], Op.not_equal, 1.0, -112, 1)
+    sel(a("BD"), a("BD"), [[-16, 8], [0, 16]], Op.is_ge, 0.0, 0, 1)
+    sel(a("BD"), a("BD"), [[16, 8], [0, 16]], Op.is_ge, 0.0, 15, -1)
     sel(a("IB"), a("IB"), [[-1, 144]], Op.is_equal, 0.0, 15, 1)
     sel(a("B8"), a("B8"), [[-16, 8]], Op.is_ge, 0.0, 0, 1)
     sel(a("WB", s(15, 143, 16)), a("B8"), [[16, 8]], Op.is_ge, 0.0, 15, -1)
-    fills()
+    sel(a("TM"), a("BD"), [[-1, 128]], Op.is_gt, 0.0, 0, 1)
+    ts(a("rj"), a("ri"), 15, Op.bitwise_and)
+    cp(scol, a("rj", s(0, 1)))
+    ts(a("lj"), a("U"), scol, Op.add)
+    ts(a("lb"), a("lj"), 16.0, Op.mult)
+    for nu, x in lists.items():
+        c, o = s(0, nu), s(x, x + nu)
+        ts(a("lq", o), a("lj", c), -(nu - 1) / 2.0, Op.add, 1.0 / nu, Op.mult)
+        ts(a("la", o), a("lq", o), 1.0 - 16.0 * nu, Op.mult)
+        tt(a("la", o), a("la", o), a("lb", c), Op.add)
+        cp(a("LS", o), a("la", o))
+    for name, segs in (("crow0", [(every, "first")]), ("crow1", [(own, "own"), (near, "near"), (far, "far")])):
+        ms(a(name, (0, 1)), -8 * BIG)
+        for seg, m in segs:
+            ms(a(name, (0, 1), s(*seg), s(16 - CFG[m], 16)), 0.0)
+    ts(a("M16"), a("U16"), scol, Op.is_equal, -2.0, Op.mult)
+    ts(a("m16"), a("M16", s(0, 16)), -128.0, Op.mult)
+    scan(a("w16"), a("h16"), a("h16"), 0.5, Op.mult, Op.min)
+    tt(a("v16"), a("w16"), a("M16", s(0, 16)), Op.mult)
+    op("v", lambda: g.vector.tensor_reduce(T.wj[:, 0:1], T.v16[:], Ax.X, Op.add), a("wj"), [a("v16")])
+    ts(a("BJ"), a("BD"), a("wj", s(0, 1)), Op.mult, -0.5, Op.mult)
+    ts(a("WW"), a("WB"), wcol, Op.mult, 1.0 / BIG, Op.mult)
+    ts(a("BW"), a("BD"), wcol, Op.mult, 1.0 / 8192, Op.mult)
+    ts(a("DO"), a("lj"), 4.0 * L, Op.add)
+    ts(a("DU"), a("lj"), float(W), Op.add, 1.0 / 512, Op.mult)
+    ts(a("CC"), a("c0"), scol, Op.subtract)
     act(a("NB"), a("IB"), scale=-1.0)
-    iota(a("K"), [[2048, 392]], 2047, 0)
+    act(a("I8"), I, scale=8192.0)
+    act(a("N8"), I, scale=-8192.0)
+    act(a("WH"), a("WB"), scale=0.5 / BIG)
+    act(a("TM"), a("TM"), scale=-1.0)
+    for k in range(16):
+        act(selk(k), a("BD"), scale=a("m16", s(k, k + 1)))
+    for r in range(RO):
+        for j in range(N):
+            iota(a("W%d" % r, s(L * j, L * j + C)), [[0, C]], 1, 0)
+    aside[0] = False
 
-    def late_constants():
-        sel(a("BD"), a("BD"), [[-16, 8], [0, 16]], Op.is_ge, 0.0, 0, 1)
-        sel(a("BD"), a("BD"), [[16, 8], [0, 16]], Op.is_ge, 0.0, 15, -1)
-        sel(a("TM"), a("BD"), [[-1, 128]], Op.is_gt, 0.0, 0, 1)
-        iota(row(1), [[0, 8], [1, 16]], 0, 0)
-        iota(row(2), [[0, 8], [-256, 16]], 0, 0)
-        sel(a("SEL"), a("SEL"), [[-1, 16], [-16, 8], [0, 16]], Op.is_equal, 0.0, 0, 1)
-        iota(a("c0"), [[L, 4], [-16, 24]], -4 * L - 1, 0)
-
-    def last_constants():
-        sel(a("SH"), a("SH"), [[-1, 128]], Op.is_equal, 0.0, 16, 1)
-        sel(a("SH"), a("SH"), [[-1, 128]], Op.not_equal, 1.0, -112, 1)
-        swap(1)
-
-    def small_constants():
-        ms(a("RM"), 1.0)
-        ms(row(0), 0.0); ms(a("rows", (0, 2), s(128, 256)), 1.0 / 8192); ms(row(4), -23.0); ms(row(5), 44.5)
-        ts(a("m2"), a("U", s(0, 16)), 1.0 / 16, Op.mult, scol, Op.is_gt)
-        ts(a("DU"), a("lj"), float(W), Op.add, 1.0 / 512, Op.mult)
-
-    def scalar_constants():
-        act(a("I8"), I, scale=8192.0)
-        act(a("WH"), a("WB"), scale=0.5 / BIG)
-        act(a("TM"), a("TM"), scale=-1.0)
-        act(a("N8"), I, scale=-8192.0)
-        for k in range(1, 16):
-            act(a("LT", s(128 * k - 128, 128 * k)), a("BD"), scale=a("m2", s(k, k + 1)))
-
-    def round_constants():
-        w = a("wcol", s(0, 1))
-        return [[lambda: ts(a("WW"), a("WB"), w, Op.mult, 1.0 / BIG, Op.mult),
-                 lambda: ts(a("BW"), a("BD"), w, Op.mult, 1.0 / 8192, Op.mult)],
-                [lambda: ts(a("RM", s(0, 96, 24)), a("RM", s(0, 96, 24)), 0.0, Op.mult),
-                 lambda: ts(a("CC"), a("c0"), scol, Op.subtract),
-                 lambda: ts(a("DO"), a("lj"), 4.0 * L, Op.add)],
-                [lambda: ms(a("crow", s(16 * own[0] + 3, 16 * own[1], 4)), 0.0), lambda: make_list(6)],
-                [lambda: make_list(18)]]
+    def phi(seg):
+        return a("PHI", s(seg[0] // 2, seg[1] // 2))
 
     def unpack(src, seg, sh):
-        u0, u1 = seg
-        au = a("AU" if sh else "A", s(16 * u0, 16 * u1))
+        au = a("AU" if sh else "A", cols(seg))
         ts(au, src, MAGIC, Op.add, -MAGIC, Op.add)
-        tt(a("PHI", s(u0 // 2, u1 // 2)), src, au, Op.subtract)
+        tt(phi(seg), src, au, Op.subtract)
 
-    def names_pe(seg, sh):
-        u0, u1 = seg
-        b, c = s(u0 // 2, u1 // 2), s(16 * u0, 16 * u1)
+    def names(seg, sh):
+        b, c, nu = s(seg[0] // 2, seg[1] // 2), cols(seg), seg[1] - seg[0]
         for h2 in range(2):
             for h in range(2):
                 k = 512 * sh + 256 * h + 128 * h2
                 mm(a("NS", b, h2), a("SW", s(k, k + 128)), a("PHI", b, h), h == 0, h == 1)
         if sh:
-            mm(a("b6", c), a("SH"), a("AU", c), True, False)
-            mm(a("b6", c), a("SH"), a("PHI", b), False, True)
             mm(a("b7", c), a("SH"), a("AU", c), True, True)
-            act(a("P", c), a("b6", c))
             act(a("A", c), a("b7", c))
-
-    def names_v(seg):
-        u0, u1 = seg
-        b, c, nu = s(u0 // 2, u1 // 2), s(16 * u0, 16 * u1), u1 - u0
         op("v", lambda: g.vector.transpose(ap(a("NT", c)), ap(a("NS", b))), a("NT", c), [a("NS", b)])
         ts(a("OFF", c), ix(a("NT", c), a("LS", s(lists[nu], lists[nu] + nu))), 2047.0, Op.add)
 
     bank = [0]
 
-    def compare(seg):
-        u0, u1 = seg
-        nu, c, z = u1 - u0, s(16 * u0, 16 * u1), a("Z", s(0, W))
-        w = 16 * nu
-        off = lambda p: a("OFF", s(16 * u0 + nu * p, 16 * u0 + nu * (p + 1)))
-        at0 = lambda p: 1728 + w * (p // 2) if nu == 6 else w * SROWS.index(p)
-        vb = lambda p: a("VB", s(at0(p), at0(p) + w))
-        at = {}
+    def compare(plan_):
+        steps = plan_.split()
+        for i, st in enumerate(steps):
+            seg, p0, p1 = {"a": every, "o": own, "n": near, "f": far}[st[1]], int(st[2], 17), int(st[3], 17)
+            nu, c, m = seg[1] - seg[0], cols(seg), p1 - p0
+            w = 16 * nu
+            off = lambda x, y: a("OFF", s(16 * seg[0] + nu * x, 16 * seg[0] + nu * y))
+            vb = lambda x, y: a("VB", s(256 * seg[0] + w * x, 256 * seg[0] + w * y))
+            if st[0] == "V":
+                for p in [int(x, 16) for x in st[2:]]:
+                    tt(a("CMP", c, p), ix(z, off(p, p + 1)), a("A", c), Op.is_ge)
+            elif st[0] == "S":
+                nm = "b%d" % (1 + bank[0] % 3)
+                bank[0] += 1
+                act(vb(p0, p1), ix(z, off(p0, p1)))
+                for k in range(m):
+                    mm(a(nm, s(k, w * m, m)), I, vb(p0 + k, p0 + k + 1), True, False)
+                    mm(a(nm, s(k, w * m, m)), NI, a("A", c), False, True)
+                act(a("CMP", c, s(p0, p1)), a(nm, s(0, w * m)), Fn.Sign, bias=0.25)
+            else:
+                for k in range(16):
+                    mm(a("CP", s(16 * seg[0] + p0, 16 * seg[1], p1)), a("WB", s(15 - k, 143 - k)),
+                       a("CMP", s(16 * seg[0] + k, 16 * seg[1], 16), s(p0, 16, p1)), False, i == len(steps) - 1 and k == 15)
 
-        def V(*ps):
-            for p in ps:
-                tt(a("CMP", c, p), ix(z, off(p)), a("P", c), Op.is_ge)
+    def open_round(r):
+        aside[0] = True
+        mm(a("CP", full), one1(128), a("crow1" if r else "crow0", (0, 1)), True, False)
+        dma("y", a("NK"), a("K", s(1, L + 1)), "keys")
+        aside[0] = False
 
-        def G(*ps):
-            for p in ps:
-                act(vb(p), ix(z, off(p)))
+    def add_names(seg, i):
+        dma("g", a("NK", cols(seg)), a("NT", cols(seg)), "acc%d" % i, accum_op=Op.add)
 
-        def D(*ps):
-            nm = "b%d" % (1 + bank[0] % 3); bank[0] += 1
-            for i, p in enumerate(ps):
-                at[p] = a(nm, s(w * i, w * i + w))
-                mm(at[p], I, vb(p), True, False)
-                mm(at[p], a("NB", s(15, 143)), a("A", c), False, True)
-
-        def S(*ps):
-            for p in ps:
-                act(a("CMP", c, p), at[p], Fn.Sign, bias=0.25)
-
-        def Cn(p0, st, stop=False, x=u0, y=u1):
-            for k in range(16):
-                mm(a("CP", s(16 * x + p0, 16 * y, st)), a("WB", s(15 - k, 143 - k)),
-                   a("CMP", s(16 * x + k, 16 * y, 16), s(p0, 16, st)), False, stop and k == 15)
-
-        return V, G, D, S, Cn
-
-    def compare_many(seg):
-        V, G, D, S, Cn = compare(seg)
-        G(1); D(1); G(5); D(5); S(1); G(9); D(9); S(5); V(0, 4, 8, 12); G(13); Cn(0, 4, False, 0, 24); D(13); S(9)
-        G(11); D(11); S(13); G(15); Cn(1, 4); D(15); V(2, 6, 10, 14); Cn(2, 4); S(11, 15); V(3, 7); Cn(3, 4, True)
-
-    def open_counts():
-        mm(a("CP", s(0, L)), one1(128), a("crow", (0, 1)), True, False)
-
-    def add_places():
-        dma("g", a("NT"), a("K", s(1, L + 1)), "acc", accum_op=Op.add)
-
-    def arrived(r):
-        for src in range(N):
-            if src != q:
-                x = C * place(q, src)
-                ops.append({"e": "x", "rd": [], "wr": a("LA%d" % r, s(x, x + C))["reg"], "sem": "ar%d_%d" % (r, src),
-                            "n": len(plan(src)[q])})
+    def arrived(r, ranks):
+        for src in ranks:
+            ops.append({"e": "x", "rd": [], "wr": a("LA%d" % r, s(C * src, C * src + C))["reg"], "sem": "ar%d_%d" % (r, src),
+                        "n": len(plan(src)[q]), "ns": 0, "after": sends[r], "aside": False,
+                        "lag": CFG["near_ns" if src in near_r else "far_ns"]})
 
     def plan(r0):
         c0 = T.cores[r0]
@@ -311,7 +289,7 @@ def rank_program(g, core, T, topo):
                 res[k] = [e for e in topo.engines(c0, T.cores[k]) if e not in few]
         return res
 
-    sent = [0]
+    sent, sends = [0], []
 
     def send(r):
         pl = plan(q)
@@ -320,164 +298,125 @@ def rank_program(g, core, T, topo):
             k = (q + 1 + j) % N
             rid, pid = topo.addr(T.cores[k], core)
             src = a("W%d" % r, s(L * j, L * j + C)); rd.append(src)
-            x = C * place(k, q)
             trs.append(RemoteDMATransfer(dst_ids=[DstId(rid=rid, pnc=pid)], dma_engine_mask=sum(1 << e for e in pl[k]),
-                                         remote_sem=T.sem["ar%d_%d" % (r, q)], src=ap(src), dst=T["LA%d" % r][:, x:x + C]))
+                                         remote_sem=T.sem["ar%d_%d" % (r, q)], src=ap(src),
+                                         dst=T["LA%d" % r][:, C * q:C * q + C]))
             sent[0] += len(pl[k])
+        sends.append(len(ops))
         op("g", lambda: g.remote_dma_fused(trs, local_sem=T.sem.sent), None, rd, "none")
 
     def settle(r):
-        full, t24, t96 = s(0, L), s(0, 24), s(0, 96)
-        extra = round_constants() if r == 0 else [[], [], [], []]
-
-        def more(k):
-            for f in extra[k]:
-                f()
-
-        for j in range(N):
-            iota(a("W%d" % r, s(L * j, L * j + C)), [[0, C]], 1, 0)
-        if r == 0:
-            scalar_constants()
-            last_constants()
-        mm(a("b7", t24), row(4), row(5, 24), True, False)
-        mm(a("b5", full), row(0), one1(L), True, False)
-        mm(a("b1", full), row(2), one1(L), True, False)
-        mm(a("b2", full), a("rows", (0, 2), s(128, 256)), a("ones", (0, 2)), True, False)
-        mm(a("b2", full), I, a("A"), False, False)
-        scan(a("S"), a("CP", full), a("NT"), 0.0, Op.max, Op.min)
+        scan(a("S"), a("CP", full), a("NK"), 0.0, Op.max, Op.min)
         tt(a("r"), a("S", s(15, L, 16)), a("K", s(0, L, 16)), Op.max)
         ts(a("x"), a("r"), W - 1, Op.bitwise_and)
-        ts(a("rk"), a("r"), 11, Op.arith_shift_right)
-        cp(a("xf"), a("x"))
         cp(a("xo"), a("x"))
-        for k in range(16):
-            mm(a("b3", s(k, L, 16)), selk(k), a("xf"), True, True)
+        ts(a("XR"), ix(a("ID"), a("xo")), 1.0 / 512, Op.mult)
         ts(a("xs"), a("x"), 1.0 / 512, Op.mult)
+        ts(a("rk"), a("r"), 11, Op.arith_shift_right)
         tt(a("kk"), a("rk"), a("U"), Op.subtract)
-        tt(a("d"), ix(a("Z", s(0, W)), a("xo")), a("A"), Op.subtract)
-        for x, y, n in pieces:
-            ts(a("XR", s(16 * y, 16 * (y + n))), a("b3", s(16 * x, 16 * (x + n))), 1.0 / (256 * 512), Op.mult)
-        more(0)
-        act(a("n"), a("d"), Fn.Relu)
-        act(a("ab"), a("kk"), Fn.Abs, bias=-68.0, scale=8.0)
-        act(a("gk"), a("ab"), bias=58.0, scale=-1.0)
+        act(a("d"), ix(z, a("xo")))
+        mm(a("b3", full), NI, a("A"), True, False)
+        mm(a("b3", full), I, a("d"), False, True)
+        act(a("n"), a("b3", full), Fn.Relu)
+        mm(a("b7", t24), row(4), row(5, 24), True, False)
         mm(a("b7", t24), a("I8"), a("kk"), False, False)
         for k in range(16):
-            mm(a("b1", s(k, L, 16)), selk(k), a("kk"), False, False)
-        mm(a("b2", full), a("BW"), a("n"), False, False)
-        for lane in range(24):
-            u = (lane - nt) % 24
-            ts(a("EQ", s(400 * lane, L * (lane + 1))), a("XR", s(16 * lane, L)), a("xs", s(u, u + 1)), Op.is_equal)
-            if lane < 23:
-                mm(a("b5", s(16 * lane + 16, L)), a("BD"), a("EQ", s(400 * lane + 16, L * (lane + 1))), False, False)
-            if lane == 2:
-                for k in range(16):
-                    mm(a("b7", t24), a("WW", s(15 - k, 143 - k)), a("n", s(k, L, 16)), False, k == 15)
-                act(a("q1"), a("b7", t24), bias=MAGIC, scale=1.0 / 2048)
-                act(a("nq"), a("q1"), bias=(MAGIC - 1) / 1024, scale=-1.0 / 1024)
-        for k in range(1, 16):
-            mm(a("b5", s(k, L, 16)), a("LT", s(128 * k - 128, 128 * k)), a("EQ", s(k, 24 * L, 400)), False, k == 15)
+            mm(a("b7", t24), a("WW", s(15 - k, 143 - k)), a("n", s(k, L, 16)), False, k == 15)
+        act(a("q1"), a("b7", t24), bias=MAGIC, scale=1.0 / 2048)
+        act(a("nq"), a("q1"), bias=(MAGIC - 1) / 1024, scale=-1.0 / 1024)
+        aside[0] = True
+        for seg in ([near, far] if r else [every]):
+            mm(a("b6", cols(seg)), a("SH") if r else I, a("AU" if r else "A", cols(seg)), True, False)
+            mm(a("b6", cols(seg)), a("SH") if r else I, phi(seg), False, True)
+            act(a("P", cols(seg)), a("b6", cols(seg)))
+        act(a("ab"), a("kk"), Fn.Abs, bias=-68.0, scale=8.0)
+        act(a("gk"), a("ab"), bias=58.0, scale=-1.0)
         ts(a("ci"), a("b7", t24), 1023.5 + 3 - q, Op.add)
-        more(1)
         ts(a("rel"), a("ci"), N - 1, Op.bitwise_and)
         tt(a("e"), a("rel"), a("gk"), Op.min)
         tt(a("ex"), a("e"), a("xs"), Op.subtract)
-        ts(a("lose"), a("b5", full), 0.5, Op.is_gt)
-        more(2)
+        mm(a("b5", full), a("BJ"), a("M16"), True, False)
+        mm(a("b1", full), row(2), one1(L), True, False)
+        mm(a("b2", full), a("rows", (0, 2), s(128, 256)), a("ones", (0, 2)), True, False)
+        mm(a("b2", full), I, a("A"), False, False)
+        mm(a("b2", full), a("BW"), a("n"), False, False)
         for k in range(16):
+            mm(a("b1", s(k, L, 16)), selk(k), a("kk"), False, False)
             mm(a("b2", s(k, L, 16)), selk(k), a("nq"), False, False)
-        mm(a("b6", t24), row(0), one1(24), True, False)
-        for x, y, n in pieces:
-            mm(a("b6", s(y, y + n)), I, a("e", s(x, x + n)), False, False)
+        mm(a("b3", t96), I, a("CC"), True, False)
+        mm(a("b7", t24), I, a("DO"), True, False)
+        aside[0] = False
+        for u in range(24):
+            ts(a("EQ", u, s(0, L - 16 * u)), a("XR", s(16 * u, L)), a("xs", s(u, u + 1)), Op.is_equal)
+            if u < 23:
+                mm(a("b5", s(16 * u + 16, L)), a("BD"), a("EQ", u, s(16, L - 16 * u)), False, False)
+        mm(a("b5", full), a("BJ"), a("EQ", t24, s(0, 16)), False, True)
+        ts(a("lose"), a("b5", full), 0.0, Op.is_ge)
         for k in range(16):
-            mm(a("b6", t24), a("WH", s(15 - k, 143 - k)), a("lose", s(k, L, 16)), False, k == 15)
-        for nm, m in (("b1", "I8"), ("b2", "N8")):
-            for x, y, n in pieces:
-                mm(a(nm, s(16 * x, 16 * (x + n))), a(m), a("lose", s(16 * y, 16 * (y + n))), False, x + n == 24)
+            mm(a("b6", t24), a("WH", s(15 - k, 143 - k)), a("lose", s(k, L, 16)), k == 0, False)
+        mm(a("b6", t24), I, a("e"), False, True)
         for j in range(N):
             ts(a("ind", s(24 * j, 24 * j + 24)), a("b6", t24), float(j), Op.is_equal if j < N - 1 else Op.is_ge)
-        for x, y, n in pieces:
-            tt(a("y", s(x, x + n)), a("b6", s(y, y + n)), a("ex", s(x, x + n)), Op.subtract)
         scan(a("sc"), a("RM"), a("ind"), 0.0, Op.mult, Op.add)
-        mm(a("b5", t96), I, a("CC"), True, False)
-        mm(a("b5", t96), a("TM"), a("ind"), False, False)
-        mm(a("b5", t96), a("BD"), a("sc"), False, True)
+        mm(a("b3", t96), a("TM"), a("ind"), False, False)
+        mm(a("b3", t96), a("BD"), a("sc"), False, True)
+        mm(a("b1", full), a("I8"), a("lose"), False, True)
+        mm(a("b2", full), a("N8"), a("lose"), False, True)
         tt(a("T1"), a("P"), a("b1", full), Op.min)
-        tt(a("prod"), a("ind"), a("b5", t96), Op.mult)
-        for x, y, n in pieces:
-            mm(a("b7", s(x, x + n)), I, a("DO", s(y, y + n)), True, False)
-            for j in range(N):
-                mm(a("b7", s(x, x + n)), I, a("prod", s(24 * j + y, 24 * j + y + n)), False, j == N - 1)
+        tt(a("prod"), a("ind"), a("b3", t96), Op.mult)
+        for j in range(N):
+            mm(a("b7", t24), I, a("prod", s(24 * j, 24 * j + 24)), False, j == N - 1)
         tt(a("T2"), a("A"), a("b2", full), Op.min)
         cp(a("slot"), a("b7", t24))
-        tt(a("y2"), a("y"), a("DU"), Op.min)
         tt(ix(a("W%d" % r), a("slot")), a("T1"), a("T2"), Op.max)
-        ts(a("so"), a("y2"), 512.0, Op.mult)
         send(r)
-        return extra[3]
+        tt(a("y"), a("b6", t24), a("ex"), Op.subtract)
+        tt(a("y2"), a("y"), a("DU"), Op.min)
+        ts(a("so"), a("y2"), 512.0, Op.mult)
 
     def pay():
         cp(ix(a("Z"), a("so")), a("n"))
 
-    small_constants()
     ts(a("PHI"), a("bil"), -2047.0, Op.add, 1.0 / 8192, Op.mult)
-    names_pe((0, 24), 0)
-    mm(a("b6", s(0, L)), I, a("A"), True, False)
-    mm(a("b6", s(0, L)), I, a("PHI"), False, True)
-    act(a("P"), a("b6", s(0, L)))
-    names_v((0, 24))
-    add_places()
-    late_constants()
-    open_counts()
-    compare_many((0, 24))
-    left = settle(0)
-    oc, fc = s(16 * own[0], 16 * own[1]), s(16 * far[0], 16 * far[1])
-    for r in range(1, RO):
-        mine = a("W%d" % (r - 1), s(3 * L, 3 * L + C))
-        act(a("P", oc), mine)
+    names(every, 0)
+    open_round(0)
+    add_names(every, 0)
+    compare(CFG["start"])
+    settle(0)
+    for r in range(1, RO + 1):
+        mine, land = a("W%d" % (r - 1), s(3 * L, 3 * L + C)), lambda seg: a("LA%d" % (r - 1), cols(seg))
+        if r == RO:
+            break
         unpack(mine, own, 0)
-        names_pe(own, 0)
-        open_counts()
         pay()
-        names_v(own)
-        for f in left:
-            f()
-        V, G, D, S, Cn = compare(own)
-        G(1, 3, 5, 7); D(1, 3, 5, 7); G(9, 11, 13, 15); D(9, 11, 13, 15); S(1, 3, 5, 7); S(9, 11, 13, 15)
-        V(2, 6, 10, 14)
-        arrived(r - 1)
-        unpack(a("LA%d" % (r - 1), fc), far, 1)
-        names_pe(far, 1)
-        V(0, 4, 8, 12)
-        Cn(2, 4)
-        Cn(1, 2)
-        names_v(far)
-        add_places()
-        compare_many(far)
-        left = settle(r)
+        names(own, 0)
+        open_round(r)
+        for i, (seg, ranks) in enumerate(((near, near_r), (far, far_r))):
+            arrived(r - 1, ranks)
+            unpack(land(seg), seg, 1)
+            names(seg, 1)
+            add_names(far if i else home, i)
+        compare(CFG["later"])
+        act(a("P", cols(own)), mine)
+        settle(r)
+    for seg, ranks in ((far, far_r), (near, near_r), (own, [])):
+        src, c = land(seg) if ranks else mine, cols(seg)
+        arrived(RO - 1, ranks)
+        unpack(src, seg, 1)
+        ts(a("YE", c), phi(seg), 8192.0, Op.mult, 2047.0, Op.add)
+        for eng, out, name in (("s", T.ya, "AU"), ("y", T.ye, "YE")):
+            for x, y, n in (((0, 16, 112), (112, 0, 16)) if ranks else ((0, 0, 128),)):
+                dma(eng, out[y:y + n, c], a(name, (x, x + n), c), "out")
     pay()
     for i in range(2):
-        dma("ys"[i], T.yz[:, 1024 * i:1024 * i + 1024], a("Z", s(1024 * i, 1024 * i + 1024)), "o%d" % i)
-    mine = a("W%d" % (RO - 1), s(3 * L, 3 * L + C))
-    unpack(mine, own, 0)
-    cp(a("YA", oc), a("A", oc))
-    ts(a("YE", oc), a("PHI", s(own[0] // 2, own[1] // 2)), 8192.0, Op.mult, 2047.0, Op.add)
-    arrived(RO - 1)
-    unpack(a("LA%d" % (RO - 1), fc), far, 1)
-    mm(a("b7", fc), a("SH"), a("AU", fc), True, True)
-    mm(a("b6", fc), a("SH"), a("PHI", s(far[0] // 2, far[1] // 2)), True, True)
-    act(a("YA", fc), a("b7", fc))
-    ts(a("YE", fc), a("b6", fc), 8192.0, Op.mult, 2047.0, Op.add)
-    for i, (x, y, n) in enumerate(pieces):
-        dma("s", T.ya[:, 16 * y:16 * (y + n)], a("YA", s(16 * x, 16 * (x + n))), "o%d" % (4 + i))
-        dma("y", T.ye[:, 16 * y:16 * (y + n)], a("YE", s(16 * x, 16 * (x + n))), "o%d" % (6 + i))
+        dma("ys"[i], T.yz[:, 1024 * i:1024 * i + 1024], a("Z", s(1024 * i, 1024 * i + 1024)), "out")
 
     def meet(xs, ys):
         return any(x[0] == y[0] and x[1] & y[1] for x in xs for y in ys)
 
     by = {}
     for i, o in enumerate(ops):
-        o["dep"] = {}
+        o["wait"], o["pre"], o["post"] = [], {}, []
         cand = set()
         for x in o["rd"] + o["wr"]:
             cand.update(by.get(x[0], []))
@@ -490,22 +429,60 @@ def rank_program(g, core, T, topo):
             else:
                 hit = meet(o["rd"], real) or meet(o["wr"], p["rd"] + p["wr"])
             if hit and p["sem"] != "none" and o["e"] != "x":
-                key = p["sem"] or "e" + p["e"]
-                o["dep"][key] = max(o["dep"].get(key, -1), j)
+                o["wait"].append(p)
+                o["pre"][j] = CFG["hop"] + (CFG["dma"] if p["sem"] and p["e"] != "x" else 0)
+            elif same and o["e"] == "t" and meet(o["wr"], p["wr"]):
+                o["pre"][j] = 0
+        if o["e"] == "x":
+            o["pre"][o["after"]] = o["lag"]
+        for j in o["pre"]:
+            ops[j]["post"].append(o)
         for x in set(x[0] for x in o["rd"] + o["wr"]):
             by.setdefault(x, []).append(i)
-    seen = {e: {} for e in Q}
+
+    for i, o in reversed(list(enumerate(ops))):
+        o["rank"] = (min([p["rank"] for p in o["post"]] + [len(ops)]) - 1e-4) if o["aside"] else i
+        o["left"], o["ready"], o["no"] = len(o["pre"]), 0, i
+    pool, free, done = {e: [] for e in "vstgyx"}, {e: 0 for e in "vstgyx"}, []
     for o in ops:
-        if o["e"] != "x":
-            o["dep"] = {k: j for k, j in o["dep"].items() if j > seen[o["e"]].get(k, -1)}
-            seen[o["e"]].update(o["dep"])
-            for j in o["dep"].values():
-                ops[j]["sig"] = True
-    count = {}
+        if not o["left"]:
+            pool[o["e"]].append(o)
+    while len(done) < len(ops):
+        t, e = min((max(free[e], min(o["ready"] for o in pool[e])), e) for e in pool if pool[e])
+        line = sorted(pool[e], key=lambda o: o["rank"])
+        pick = None
+        for k, o in enumerate(line):
+            if o["ready"] <= t and not any(p["ready"] - t < CFG["patience"].get(e, 1) * (t + o["ns"] - p["ready"]) for p in line[:k]):
+                pick = o
+                break
+        if pick is None:
+            free[e] = min(o["ready"] for o in line if o["ready"] > t)
+            continue
+        pool[e].remove(pick)
+        pick["t"], free[e] = t, t + pick["ns"]
+        for o in pick["post"]:
+            o["left"] -= 1
+            o["ready"] = max(o["ready"], free[e] + o["pre"][pick["no"]])
+            if not o["left"]:
+                pool[o["e"]].append(o)
+        done.append(pick)
+    ops = done
+
+    seen = {e: {} for e in "vstgyx"}
+    for i, o in enumerate(ops):
+        o["i"], o["dep"] = i, {}
+        for p in o["wait"]:
+            key = p["sem"] or "e" + p["e"]
+            if p["i"] > max(seen[o["e"]].get(key, -1), o["dep"].get(key, -1)):
+                o["dep"][key] = p["i"]
+        seen[o["e"]].update(o["dep"])
+        for j in o["dep"].values():
+            ops[j]["sig"] = True
+    total = {}
     for o in ops:
         key = o["sem"] or "e" + o["e"]
         if o["e"] == "x":
-            count[key] = o["at"] = o["n"]
+            total[key] = o["at"] = o["n"]
             continue
         for k, j in o["dep"].items():
             Q[o["e"]].wait_ge(T.sem[k], ops[j]["at"])
@@ -515,7 +492,7 @@ def rank_program(g, core, T, topo):
         if o["sem"] or o.get("sig"):
             n = 16 if o["sem"] else 1
             ins.then_inc(T.sem[key], n)
-            count[key] = o["at"] = count.get(key, 0) + n
-    count["sent"] = sent[0]
-    for k, n in count.items():
+            total[key] = o["at"] = total.get(key, 0) + n
+    total["sent"] = sent[0]
+    for k, n in total.items():
         g.wait_ge(T.sem[k], n)

@@ -6,28 +6,29 @@ MAGIC = 12582912.0
 BIG = 1048576.0
 f32, bf, f16, i32, u16 = "float32", "bfloat16", "float16", "int32", "uint16"
 CYCLE = 0.83
-CFG = {"issue": 100, "pe": 0.45, "gather": 1.56, "scatter": 3.8, "fix": 20, "hop": 180, "dma": 2000, "near_ns": 2600, "far_ns": 3600,
-       "patience": {"v": 1.2, "s": 0, "t": 0}, "first": 6, "own": 10, "near": 7, "far": 6,
-       "start": "Sacd Sade Saef Saab Safg Sabc Va048 Ca04 Va159 Ca14 Va26 Ca24 Va37 Ca34",
-       "later": "Socg So8c So68 Vo012345 Sncg Sn9c Vn012345678 Sfce Sfeg Sfab Sfbc Co01 Cn01 Vf048 Cf04 Vf159 Cf14 Vf26 Cf24 Vf37 Cf34"}
+CFG = {"issue": 100, "pe": 0.45, "gather": 1.56, "scatter": 3.8, "fix": 20, "hop": 200, "dma": 2000, "lag": [2400, 3300, 3300],
+       "patience": {"v": 1.2, "s": 0, "t": 0, "u": 3}, "cut": 1536, "banks": "b1 b2 b3", "prep": "nf", "late_c": False, "soon": 0, "ahead": 4, "paced": "", "bw": True, "split": False, "comb": False,
+       "start": "Sheg Shce Shac Sh9a Vh02468 Ch02 Vh1357 Ch12 Sfce Sfeg Sfab Sfbc Vf048 Cf04 Vf159 Cf14 Vf26 Cf24 Vf37 Cf34",
+       "later": "Socg So8c Vo01234567 Sncg Sn9c Vn012345678 Sfef Sfcd Sfab Sfde Sffg Sfbc Co01 Cn01 Vf02468 Cf02 Vf159 Cf14 Vf37 Cf34"}
 
 
 def sb(n, d):
     return ("sbuf", [128] + (n if isinstance(n, list) else [n]), d)
 
 
-SCRATCH = {"PHI": sb([12, 2, 16], f16), "CMP": sb([L, 16], bf), "NS": ("psum", [128, 16, 2, 16], f32),
+SCRATCH = {"PHI": sb([12, 2, 16], f16), "CMP": sb([L, 16], bf), "A32": sb(L, bf), "AL": sb(L, bf), "NS": ("psum", [128, 16, 2, 16], f32),
            "CP": ("psum", [128, 512], f32), "EQ": sb([24, L], bf), "crow0": sb([24, 16], bf), "crow1": sb([24, 16], bf)}
-for _d, _l in ((f32, "P NT NK S T1 T2 ab:24 gk:24 xs:24 ex:24 y:24 y2:24 DU:24 q1:24 YE col:8 K:392 U:24 c0:96 lj:24 lb:24 "
-                     "la:48 ID:2048 h16:16 w16:16 v16:16 m16:16 wj:8"),
-               (bf, "A Z:2432 wcol:16 AU VB:6144 d n lose kk:24 e:24 nq:24 ind:96 sc:96 B8:8 WB:144 WW:144 WH:144 U16 M16 "
-                    "BD:128 BW:128 BJ:128 TM:128 IB:144 NB:144 I8:128 N8:128 SH:128 SW:1024 SEL:2048 ones rows:768 RM:96"),
-               (i32, "bil r:24 x:24 rk:24 ci:24 rel:24 ri:8 rj:8 lq:48"),
-               (f16, "prod:96 XR CC:96 DO:24"),
+for _d, _l in ((f32, "Z:2432 n32 P NT NK S T1 T2 ab:24 gk:24 xs:24 ex:24 y:24 y2:24 DU:24 q1:24 YE col:8 gcol:8 K:392 U:24 c0:120 R5:120 pick:120 lj:24 lb:24 "
+                     "SH32:128 I32:128 la:48 ID:2048 h16:16 w16:16 v16:16 m16:16 wj:8"),
+               (bf, "A ZB:2048 wcol:16 AU VB:6144 d n kk:24 e:24 nq:24 ind:96 sc:96 B8:8 WB:144 WW:144 WH:144 U16 M16 "
+                    "G8:128 BD:128 BW:128 BJ:128 TM:128 IB:128 NB:128 M I4:128 N4:128 N8:128 NH:128 SH:128 SW:1024 SEL:2048 ones rows:768 RM:96"),
+               (i32, "bil r:24 x:24 rk:24 ci:24 rel:24 ri:8 rj:8 rg:8 lq:48"),
+               (f16, "XR CC:120"),
                (u16, "OFF xo:24 so:24 slot:24 LS:96")):
     for _n in _l.split():
         SCRATCH[_n.split(":")[0]] = sb(int(_n.split(":")[1]) if ":" in _n else L, _d)
-for _n in ("b1", "b2", "b3", "b5", "b6", "b7"):
+SCRATCH.update(hits=("psum", [128, 32, 16], f32), lose=sb([24, 16], bf))
+for _n in ("b1", "b2", "b3", "b6", "b7"):
     SCRATCH[_n] = ("psum", [128, 512], f32)
 for _r in range(RO):
     SCRATCH["W%d" % _r] = sb(5 * L, f32)
@@ -40,7 +41,7 @@ def rank_program(g, core, T, topo):
     q = T.rank_of(core)
     if q is None:
         return
-    ops, aside = [], [False]
+    ops, aside, urgent, gate = [], [False], [False], [None]
     Q = {"v": g.vector, "s": g.scalar, "t": g.tensor, "g": g, "y": g.sync}
 
     def a(name, *idx):
@@ -70,7 +71,7 @@ def rank_program(g, core, T, topo):
             return CFG["issue"]
         n, x = out["n"], (ins or [out])[0]
         if eng == "t":
-            return max(64, n) * CFG["pe"]
+            return max(64, n) * CFG["pe"] * (1 if x["two"] else 4)
         if eng == "g":
             return 150 + 2 * n * CYCLE
         if "off" in out or "off" in x:
@@ -87,7 +88,8 @@ def rank_program(g, core, T, topo):
                     wr += [(n, m, "ps") for n, m in x["reg"]]
         if isinstance(out, dict):
             wr += out["reg"]; rd += out.get("off", [])
-        ops.append({"e": eng, "fn": fn, "rd": rd, "wr": wr, "sem": sem, "ns": span(eng, out, ins, sem, both), "aside": aside[0]})
+        ops.append({"e": eng, "fn": fn, "rd": rd, "wr": wr, "sem": sem, "ns": span(eng, out, ins, sem, both), "aside": aside[0],
+                    "urgent": urgent[0], "gate": gate[0] if aside[0] else None})
 
     def tt(out, x, y, o):
         op("v", lambda: g.vector.tensor_tensor(ap(out), ap(x), ap(y), o), out, [x, y], both=True)
@@ -127,7 +129,7 @@ def rank_program(g, core, T, topo):
         op(eng, lambda: Q[eng].dma_start(ap(out), ap(x), **kw), out, ins, sem)
 
     scol, wcol = a("col", s(0, 1)), a("wcol", s(0, 1))
-    I, NI = a("IB", s(15, 143)), a("NB", s(15, 143))
+    I, NI = a("IB"), a("NB")
     one1 = lambda n: a("ones", (0, 1), s(0, n))
     row = lambda k, n=128: a("rows", (0, 1), s(128 * k, 128 * k + n))
     selk = lambda k: a("SEL", s(128 * k, 128 * k + 128))
@@ -137,43 +139,49 @@ def rank_program(g, core, T, topo):
     far_r = [k for k in range(N) if k != q and k not in near_r]
     own, near, far = [(6 * min(k), 6 * max(k) + 6) for k in ([q], near_r, far_r)]
     every, home = (0, 24), (min(own[0], near[0]), max(own[1], near[1]))
+    far_r.sort(key=lambda k: topo.die(T.cores[k]) != topo.die(core))
+    ranks = {"o": [], "n": near_r, "f": far_r, "x": far_r[:1], "y": far_r[1:]}
+    segs = {k: (6 * min(v), 6 * max(v) + 6) for k, v in ranks.items() if v}
+    segs.update(a=every, o=own, h=home)
     cols = lambda seg: s(16 * seg[0], 16 * seg[1])
-    lists = {24: 0, 6: 24, 12: 30}
+    lists = {12: 0, 6: 12}
 
     dma("y", a("bil"), T.bills[:], "l0")
     dma("s", a("A"), T.due[:], "l1")
-    dma("y", z, T.z0[:], "l2")
+    dma("y", a("ZB"), T.z0[:], "l2")
     op("s", lambda: g.scalar.dma_start(T.wcol[:, 0:1], T.wt[:]), a("wcol"), [], "l3")
     aside[0] = True
+    for k in range(0, W, 512):
+        act(a("Z", s(k, k + 512)), a("ZB", s(k, k + 512)), Fn.Silu, scale=32.0, bias=16.0)
+    ops[-4]["ns"] += 1300
     iota(a("ri"), [[0, 8]], 0, 1, False)
     iota(a("U"), [[16, 24]], 0, 0)
+    iota(a("G8"), [[1, 8], [0, 16]], 0, 0)
     iota(a("U16"), [[0, 24], [1, 16]], 0, 0)
     iota(a("K"), [[2048, 392]], 2047, 0)
     for k in range(0, W, 512):
         iota(a("ID", s(k, k + 512)), [[1, 512]], k, 0)
-    iota(a("c0"), [[L, 4], [-16, 24]], -4 * L - 1, 0)
-    for name, v in (("ones", 1.0), ("IB", 1.0), ("B8", BIG), ("WB", 0.0), ("h16", 0.5), ("RM", 1.0)):
+    iota(a("c0"), [[0, 24], [L, 5]], -2049, 0)
+    for name, v in (("ones", 1.0), ("B8", BIG), ("WB", 0.0), ("h16", 0.5), ("RM", 1.0)):
         ms(a(name), v)
-    ms(a("SW", s(0, 512)), 8192.0)
     ms(a("RM", s(0, 96, 24)), 0.0)
-    ms(a("rows", (0, 2), s(128, 256)), 1.0 / 8192); ms(row(4), -23.0); ms(row(5), 44.5)
-    iota(row(1), [[0, 8], [1, 16]], 0, 0)
-    iota(row(2), [[0, 8], [-256, 16]], 0, 0)
-    for name, x, y, v in (("BD", 0, 128, 1.0), ("SH", 0, 128, 1.0), ("SW", 512, 768, 8192.0), ("SW", 768, 1024, 8192.0)):
-        act(a(name, s(x, y)), a("ones", s(0, y - x)), scale=v)
+    ms(a("rows", (0, 2), s(128, 256)), 1.0); ms(row(4), -23.0); ms(row(5), 44.5)
+    iota(row(1), [[0, 8], [4096, 16]], 0, 0)
+    o128 = a("ones", s(0, 128))
     for sh in range(2):
         for h in range(2):
             for h2 in range(2):
                 m = a("SW", s(512 * sh + 256 * h + 128 * h2, 512 * sh + 256 * h + 128 * h2 + 128))
                 base = 16 * sh - 16 * h2 - 1000 * h
-                sel(m, m, [[-32, 4], [1000, 2], [-1, 16]], Op.is_equal, 0.0, base, 1)
+                sel(m, o128, [[-32, 4], [1000, 2], [-1, 16]], Op.is_equal, 0.0, base, 1)
                 if sh and not h2:
-                    sel(m, m, [[-32, 4], [1000, 2], [-1, 16]], Op.not_equal, 8192.0, base - 128, 1)
-    sel(a("SH"), a("SH"), [[-1, 128]], Op.is_equal, 0.0, 16, 1)
+                    sel(m, m, [[-32, 4], [1000, 2], [-1, 16]], Op.not_equal, 1.0, base - 128, 1)
+    sel(a("SH"), o128, [[-1, 128]], Op.is_equal, 0.0, 16, 1)
     sel(a("SH"), a("SH"), [[-1, 128]], Op.not_equal, 1.0, -112, 1)
-    sel(a("BD"), a("BD"), [[-16, 8], [0, 16]], Op.is_ge, 0.0, 0, 1)
-    sel(a("BD"), a("BD"), [[16, 8], [0, 16]], Op.is_ge, 0.0, 15, -1)
-    sel(a("IB"), a("IB"), [[-1, 144]], Op.is_equal, 0.0, 15, 1)
+    ts(a("rg"), a("ri"), 4, Op.arith_shift_right)
+    cp(a("gcol"), a("rg"))
+    ts(a("BD"), a("G8"), a("gcol", s(0, 1)), Op.is_equal)
+    tt(I, a("SW", s(0, 128)), a("SW", s(384, 512)), Op.add)
     sel(a("B8"), a("B8"), [[-16, 8]], Op.is_ge, 0.0, 0, 1)
     sel(a("WB", s(15, 143, 16)), a("B8"), [[16, 8]], Op.is_ge, 0.0, 15, -1)
     sel(a("TM"), a("BD"), [[-1, 128]], Op.is_gt, 0.0, 0, 1)
@@ -187,82 +195,111 @@ def rank_program(g, core, T, topo):
         ts(a("la", o), a("lq", o), 1.0 - 16.0 * nu, Op.mult)
         tt(a("la", o), a("la", o), a("lb", c), Op.add)
         cp(a("LS", o), a("la", o))
-    for name, segs in (("crow0", [(every, "first")]), ("crow1", [(own, "own"), (near, "near"), (far, "far")])):
+    for name, steps in (("crow0", CFG["start"].split()), ("crow1", CFG["later"].split())):
         ms(a(name, (0, 1)), -8 * BIG)
-        for seg, m in segs:
-            ms(a(name, (0, 1), s(*seg), s(16 - CFG[m], 16)), 0.0)
+        for k in sorted({st[1] for st in steps if st[0] == "S"}):
+            ms(a(name, (0, 1), s(*segs[k]), s(min(int(st[2], 16) for st in steps if st[:2] == "S" + k), 16)), 0.0)
     ts(a("M16"), a("U16"), scol, Op.is_equal, -2.0, Op.mult)
-    ts(a("m16"), a("M16", s(0, 16)), -128.0, Op.mult)
+    ts(a("v16"), a("U", s(0, 16)), 1.0 / 16, Op.mult, scol, Op.is_equal)
+    ts(a("m16"), a("v16"), 4096.0, Op.mult)
     scan(a("w16"), a("h16"), a("h16"), 0.5, Op.mult, Op.min)
-    tt(a("v16"), a("w16"), a("M16", s(0, 16)), Op.mult)
-    op("v", lambda: g.vector.tensor_reduce(T.wj[:, 0:1], T.v16[:], Ax.X, Op.add), a("wj"), [a("v16")])
-    ts(a("BJ"), a("BD"), a("wj", s(0, 1)), Op.mult, -0.5, Op.mult)
+    tt(a("w16"), a("w16"), a("v16"), Op.mult)
+    op("v", lambda: g.vector.tensor_reduce(T.wj[:, 0:1], T.w16[:], Ax.X, Op.add), a("wj"), [a("w16")])
+    ts(a("BJ"), a("BD"), a("wj", s(0, 1)), Op.mult)
     ts(a("WW"), a("WB"), wcol, Op.mult, 1.0 / BIG, Op.mult)
-    ts(a("BW"), a("BD"), wcol, Op.mult, 1.0 / 8192, Op.mult)
-    ts(a("DO"), a("lj"), 4.0 * L, Op.add)
+    ts(a("BW"), a("BD"), wcol, Op.mult)
     ts(a("DU"), a("lj"), float(W), Op.add, 1.0 / 512, Op.mult)
-    ts(a("CC"), a("c0"), scol, Op.subtract)
-    act(a("NB"), a("IB"), scale=-1.0)
-    act(a("I8"), I, scale=8192.0)
-    act(a("N8"), I, scale=-8192.0)
+    cp(a("CC"), a("c0"))
+    cp(a("CC", s(0, 120, 5)), a("lj"))
+    ms(a("R5"), 1.0)
+    ms(a("R5", s(0, 120, 5)), 0.0)
+    ts(a("NB"), a("IB"), -1.0, Op.mult)
+    act(a("NH"), a("SH"), scale=-1.0)
+    act(a("SH32"), a("SH"))
+    act(a("I4"), I, scale=-4096.0)
+    act(a("N4"), I, scale=-4.0)
+    act(a("N8"), I, scale=-131072.0)
     act(a("WH"), a("WB"), scale=0.5 / BIG)
     act(a("TM"), a("TM"), scale=-1.0)
+    sel(a("TM"), a("TM"), [[-1, 128]], Op.not_equal, 2048.0, 0, 1)
     for k in range(16):
         act(selk(k), a("BD"), scale=a("m16", s(k, k + 1)))
+    later = [o for o in ops if o["aside"] and (o["wr"][0][0] not in ("A32", "SEL") if o["e"] == "s" else
+                                               o["wr"][0][0] in ("WW", "M16", "CC"))]
+    for o in ops:
+        o["aside"] = o["aside"] and o["wr"][0][0] not in ("ri", "U", "G8", "rg", "gcol", "BD", "rj", "col", "v16", "m16")
     for r in range(RO):
         for j in range(N):
-            iota(a("W%d" % r, s(L * j, L * j + C)), [[0, C]], 1, 0)
+            iota(a("W%d" % r, s(L * j + L, L * j + L + C)), [[0, C]], 0, 0)
     aside[0] = False
 
     def phi(seg):
         return a("PHI", s(seg[0] // 2, seg[1] // 2))
 
-    def unpack(src, seg, sh):
-        au = a("AU" if sh else "A", cols(seg))
-        ts(au, src, MAGIC, Op.add, -MAGIC, Op.add)
-        tt(phi(seg), src, au, Op.subtract)
-
-    def names(seg, sh):
+    def names(src, seg, sh):
         b, c, nu = s(seg[0] // 2, seg[1] // 2), cols(seg), seg[1] - seg[0]
+        if src:
+            ts(phi(seg), src, MAGIC, Op.add, -MAGIC, Op.add)
+        else:
+            ts(phi(seg), a("bil", c), -2047.0, Op.add)
         for h2 in range(2):
             for h in range(2):
                 k = 512 * sh + 256 * h + 128 * h2
                 mm(a("NS", b, h2), a("SW", s(k, k + 128)), a("PHI", b, h), h == 0, h == 1)
-        if sh:
-            mm(a("b7", c), a("SH"), a("AU", c), True, True)
-            act(a("A", c), a("b7", c))
+        if src and seg == far:
+            mm(a("b7", c), a("SH32"), src, True, False)
+            mm(a("b7", c), a("NH"), phi(seg), False, True)
+        elif src:
+            tt(a("AU", c), src, phi(seg), Op.subtract)
+            if sh:
+                mm(a("b7", c), a("SH"), a("AU", c), True, True)
+        if src:
+            act(a("A32", c), a("b7" if sh else "AU", c), scale=16384.0, bias=32.0)
         op("v", lambda: g.vector.transpose(ap(a("NT", c)), ap(a("NS", b))), a("NT", c), [a("NS", b)])
         ts(a("OFF", c), ix(a("NT", c), a("LS", s(lists[nu], lists[nu] + nu))), 2047.0, Op.add)
 
     bank = [0]
 
-    def compare(plan_):
-        steps = plan_.split()
+    def fetch(out, off, r):
+        if r:
+            act(out, ix(z, off), bias=-16.0)
+        else:
+            act(out, ix(a("ZB"), off))
+
+    def compare(plan_, r):
+        steps, signs = plan_.split(), []
+        bank[0] = 0
         for i, st in enumerate(steps):
-            seg, p0, p1 = {"a": every, "o": own, "n": near, "f": far}[st[1]], int(st[2], 17), int(st[3], 17)
+            seg, p0, p1 = segs[st[1]], int(st[2], 17), int(st[3:4] or "0", 17)
             nu, c, m = seg[1] - seg[0], cols(seg), p1 - p0
-            w = 16 * nu
+            w, due = 16 * nu, a("A32" if r else "A", c)
             off = lambda x, y: a("OFF", s(16 * seg[0] + nu * x, 16 * seg[0] + nu * y))
             vb = lambda x, y: a("VB", s(256 * seg[0] + w * x, 256 * seg[0] + w * y))
             if st[0] == "V":
                 for p in [int(x, 16) for x in st[2:]]:
-                    tt(a("CMP", c, p), ix(z, off(p, p + 1)), a("A", c), Op.is_ge)
+                    tt(a("CMP", c, p), ix(z if r else a("ZB"), off(p, p + 1)), due, Op.is_ge)
             elif st[0] == "S":
-                nm = "b%d" % (1 + bank[0] % 3)
+                nm = CFG["banks"].split()[bank[0] % len(CFG["banks"].split())]
                 bank[0] += 1
-                act(vb(p0, p1), ix(z, off(p0, p1)))
+                fetch(vb(p0, p1), off(p0, p1), r)
+                if len(signs) > 1 and st[1] in CFG["paced"]:
+                    ops[-1]["gate"] = signs[-2]
                 for k in range(m):
-                    mm(a(nm, s(k, w * m, m)), I, vb(p0 + k, p0 + k + 1), True, False)
-                    mm(a(nm, s(k, w * m, m)), NI, a("A", c), False, True)
+                    mm(a(nm, s(k, w * m, m)), NI, due, k == 0, False)
+                for k in range(m):
+                    mm(a(nm, s(k, w * m, m)), I, vb(p0 + k, p0 + k + 1), False, k == m - 1)
                 act(a("CMP", c, s(p0, p1)), a(nm, s(0, w * m)), Fn.Sign, bias=0.25)
+                signs.append(len(ops) - 1)
             else:
                 for k in range(16):
-                    mm(a("CP", s(16 * seg[0] + p0, 16 * seg[1], p1)), a("WB", s(15 - k, 143 - k)),
-                       a("CMP", s(16 * seg[0] + k, 16 * seg[1], 16), s(p0, 16, p1)), False, i == len(steps) - 1 and k == 15)
+                    last = not any(x[0] == "C" and (x[1] == "f") == (st[1] == "f") for x in steps[i + 1:])
+                    mm(a("CP" if st[1] == "f" else "b6", s(16 * seg[0] + p0, 16 * seg[1], p1)), a("WB", s(15 - k, 143 - k)),
+                       a("CMP", s(16 * seg[0] + k, 16 * seg[1], 16), s(p0, 16, p1)), False, last and k == 15)
 
     def open_round(r):
         aside[0] = True
-        mm(a("CP", full), one1(128), a("crow1" if r else "crow0", (0, 1)), True, False)
+        for b, seg in (("b6", home), ("CP", far)):
+            mm(a(b, cols(seg)), one1(128), a("crow1" if r else "crow0", (0, 1), s(*seg)), True, False)
         dma("y", a("NK"), a("K", s(1, L + 1)), "keys")
         aside[0] = False
 
@@ -272,151 +309,168 @@ def rank_program(g, core, T, topo):
     def arrived(r, ranks):
         for src in ranks:
             ops.append({"e": "x", "rd": [], "wr": a("LA%d" % r, s(C * src, C * src + C))["reg"], "sem": "ar%d_%d" % (r, src),
-                        "n": len(plan(src)[q]), "ns": 0, "after": sends[r], "aside": False,
-                        "lag": CFG["near_ns" if src in near_r else "far_ns"]})
+                        "n": len(few) // (1 if CFG["split"] or src in near_r else 2), "ns": 0, "urgent": False, "after": sends[r], "aside": False,
+                        "lag": CFG["lag"][(near_r + far_r).index(src)]})
 
-    def plan(r0):
-        c0 = T.cores[r0]
-        others = [k for k in range(N) if k != r0]
-        few = min((topo.engines(c0, T.cores[k]) for k in others), key=len)
-        out = [k for k in others if topo.engines(c0, T.cores[k]) == few]
-        res = {}
-        for i, k in enumerate(out):
-            m = len(few) // len(out)
-            res[k] = few[m * i:m * i + m]
-        for k in others:
-            if k not in out:
-                res[k] = [e for e in topo.engines(c0, T.cores[k]) if e not in few]
-        return res
-
+    few = topo.engines(core, T.cores[far_r[0]])
+    rest = [e for e in topo.engines(core, T.cores[near_r[0]]) if e not in few]
     sent, sends = [0], []
 
     def send(r):
-        pl = plan(q)
-        trs, rd = [], []
-        for j in range(N - 1):
-            k = (q + 1 + j) % N
-            rid, pid = topo.addr(T.cores[k], core)
-            src = a("W%d" % r, s(L * j, L * j + C)); rd.append(src)
-            trs.append(RemoteDMATransfer(dst_ids=[DstId(rid=rid, pnc=pid)], dma_engine_mask=sum(1 << e for e in pl[k]),
-                                         remote_sem=T.sem["ar%d_%d" % (r, q)], src=ap(src),
-                                         dst=T["LA%d" % r][:, C * q:C * q + C]))
-            sent[0] += len(pl[k])
         sends.append(len(ops))
-        op("g", lambda: g.remote_dma_fused(trs, local_sem=T.sem.sent), None, rd, "none")
+        for dests in ((far_r[:1] + near_r, far_r[1:]) if CFG["split"] else (far_r + near_r,)):
+            trs, rd = [], []
+            for k in dests:
+                j, eng = (k - q - 1) % N, few if k in far_r else rest
+                if not CFG["split"] and k in far_r:
+                    eng = few[far_r.index(k)::2] if CFG["comb"] else few[4 * far_r.index(k):4 * far_r.index(k) + 4]
+                rid, pid = topo.addr(T.cores[k], core)
+                src = a("W%d" % r, s(L * j + L, L * j + L + C)); rd.append(src)
+                trs.append(RemoteDMATransfer(dst_ids=[DstId(rid=rid, pnc=pid)], dma_engine_mask=sum(1 << e for e in eng),
+                                             remote_sem=T.sem["ar%d_%d" % (r, q)], src=ap(src),
+                                             dst=T["LA%d" % r][:, C * q:C * q + C]))
+                sent[0] += len(eng)
+            op("g", lambda trs=trs: g.remote_dma_fused(trs, local_sem=T.sem.sent), None, rd, "none")
 
     def settle(r):
-        scan(a("S"), a("CP", full), a("NK"), 0.0, Op.max, Op.min)
-        tt(a("r"), a("S", s(15, L, 16)), a("K", s(0, L, 16)), Op.max)
-        ts(a("x"), a("r"), W - 1, Op.bitwise_and)
-        cp(a("xo"), a("x"))
-        ts(a("XR"), ix(a("ID"), a("xo")), 1.0 / 512, Op.mult)
-        ts(a("xs"), a("x"), 1.0 / 512, Op.mult)
+        gate[0] = len(ops) - 1
+        for b, seg in (("CP", far), ("b6", home)):
+            c, u, x = cols(seg), s(*seg), 16 * seg[0]
+            scan(a("S", c), a(b, c), a("NK", c), 0.0, Op.max, Op.min)
+            tt(a("r", u), a("S", s(x + 15, x + 192, 16)), a("K", s(x, x + 192, 16)), Op.max)
+            ts(a("x", u), a("r", u), W - 1, Op.bitwise_and)
+            cp(a("xo", u), a("x", u))
+            ts(a("XR", c), ix(a("ID"), a("xo", u)), 1.0 / 512, Op.mult)
+            ts(a("xs", u), a("x", u), 1.0 / 512, Op.mult)
         ts(a("rk"), a("r"), 11, Op.arith_shift_right)
-        tt(a("kk"), a("rk"), a("U"), Op.subtract)
-        act(a("d"), ix(z, a("xo")))
-        mm(a("b3", full), NI, a("A"), True, False)
-        mm(a("b3", full), I, a("d"), False, True)
-        act(a("n"), a("b3", full), Fn.Relu)
+        tt(a("kk"), a("U"), a("rk"), Op.subtract)
+        aside[0] = True
+        mm(a("b3", full), NI, a("A32" if r else "A"), True, False)
         mm(a("b7", t24), row(4), row(5, 24), True, False)
-        mm(a("b7", t24), a("I8"), a("kk"), False, False)
+        aside[0] = False
+        for seg in (home, far):
+            fetch(a("d", cols(seg)), a("xo", s(*seg)), r)
+            mm(a("b3", cols(seg)), I, a("d", cols(seg)), False, seg == far)
+        act(a("n"), a("b3", full), Fn.Relu, scale=1.0 / 32 if r else 1.0)
+        mm(a("b7", t24), a("I4"), a("kk"), False, False)
+        aside[0] = CFG["late_c"]
         for k in range(16):
             mm(a("b7", t24), a("WW", s(15 - k, 143 - k)), a("n", s(k, L, 16)), False, k == 15)
         act(a("q1"), a("b7", t24), bias=MAGIC, scale=1.0 / 2048)
-        act(a("nq"), a("q1"), bias=(MAGIC - 1) / 1024, scale=-1.0 / 1024)
+        act(a("nq"), a("q1"), bias=(MAGIC - 1) / 2, scale=-0.5)
         aside[0] = True
-        for seg in ([near, far] if r else [every]):
-            mm(a("b6", cols(seg)), a("SH") if r else I, a("AU" if r else "A", cols(seg)), True, False)
-            mm(a("b6", cols(seg)), a("SH") if r else I, phi(seg), False, True)
-            act(a("P", cols(seg)), a("b6", cols(seg)))
-        act(a("ab"), a("kk"), Fn.Abs, bias=-68.0, scale=8.0)
+        act(a("n32"), a("b3", full), Fn.Relu, bias=16.0, scale=1.0 if r else 32.0)
+        act(a("AL"), a("A32" if r else "A"), scale=1.0 / (16384 if r else 512), bias=-1.0 / 512)
+        mm(a("NS", s(0, 12)), a("rows", (0, 2), s(128, 256)), a("ones", (0, 2)), True, False)
+        for k in range(16):
+            mm(a("NS", s(0, 12), s(0, 2), k), selk(k), a("kk"), False, False)
+        act(a("ab"), a("kk"), Fn.Abs, bias=-68.0, scale=-8.0)
         act(a("gk"), a("ab"), bias=58.0, scale=-1.0)
         ts(a("ci"), a("b7", t24), 1023.5 + 3 - q, Op.add)
+        for b, half in (("b1", (0, 12)), ("CP", (12, 24))):
+            mm(a(b, cols(half)), I, a("AL", cols(half)), True, False)
+            for seg in ([far] if half == far else [own, near]):
+                mm(a(b, cols(seg)), a("SH") if r and seg != own else I, phi(seg), False, False)
         ts(a("rel"), a("ci"), N - 1, Op.bitwise_and)
         tt(a("e"), a("rel"), a("gk"), Op.min)
         tt(a("ex"), a("e"), a("xs"), Op.subtract)
-        mm(a("b5", full), a("BJ"), a("M16"), True, False)
-        mm(a("b1", full), row(2), one1(L), True, False)
+        mm(a("hits", t24), a("BJ"), a("M16"), True, False)
         mm(a("b2", full), a("rows", (0, 2), s(128, 256)), a("ones", (0, 2)), True, False)
-        mm(a("b2", full), I, a("A"), False, False)
         mm(a("b2", full), a("BW"), a("n"), False, False)
         for k in range(16):
-            mm(a("b1", s(k, L, 16)), selk(k), a("kk"), False, False)
             mm(a("b2", s(k, L, 16)), selk(k), a("nq"), False, False)
-        mm(a("b3", t96), I, a("CC"), True, False)
-        mm(a("b7", t24), I, a("DO"), True, False)
+        mm(a("b2", full), I, a("AL"), False, False)
+        mm(a("b3", s(0, 120)), I, a("CC"), True, False)
         aside[0] = False
-        for u in range(24):
-            ts(a("EQ", u, s(0, L - 16 * u)), a("XR", s(16 * u, L)), a("xs", s(u, u + 1)), Op.is_equal)
-            if u < 23:
-                mm(a("b5", s(16 * u + 16, L)), a("BD"), a("EQ", u, s(16, L - 16 * u)), False, False)
-        mm(a("b5", full), a("BJ"), a("EQ", t24, s(0, 16)), False, True)
-        ts(a("lose"), a("b5", full), 0.0, Op.is_ge)
+        n = CFG["ahead"]
+        pairs = ([(u, u, 12) for u in range(n)] + [(u, 12, 24) for u in range(n)] + [(u, u, 24) for u in range(n, 24)] if home[0] == 0
+                 else [(u, u, 24) for u in list(range(12, 12 + n)) + list(range(12)) + list(range(12 + n, 24))])
+        diag = {17: s(0, 18), 23: s(18, 24)}
+        for u, x, y in pairs:
+            ts(a("EQ", u, s(16 * (x - u), 16 * (y - u))), a("XR", s(16 * x, 16 * y)), a("xs", s(u, u + 1)), Op.is_equal)
+            x = max(x, u + 1)
+            if x < y:
+                mm(a("hits", s(x, y)), a("BD"), a("EQ", u, s(16 * (x - u), 16 * (y - u))), False, False)
+            if u in diag and y == 24:
+                mm(a("hits", diag[u]), a("BJ"), a("EQ", diag[u], s(0, 16)), False, u == pairs[-1][0])
+        for c in (s(0, 8), s(8, 16)):
+            ts(a("lose", t24, c), a("hits", t24, c), 0.0, Op.is_ge)
         for k in range(16):
-            mm(a("b6", t24), a("WH", s(15 - k, 143 - k)), a("lose", s(k, L, 16)), k == 0, False)
+            mm(a("b6", t24), a("WH", s(15 - k, 143 - k)), a("lose", t24, k), k == 0, False)
         mm(a("b6", t24), I, a("e"), False, True)
+        urgent[0] = True
+        mm(a("NS", s(0, 12)), a("N8"), a("lose"), False, True)
+        for h in range(2):
+            act(a("M", s(192 * h, 192 * h + 192)), a("NS", s(6 * h, 6 * h + 6)), Fn.Relu, bias=2048.0)
+        mm(a("b2", full), a("N8"), a("lose"), False, True)
+        for h, b in enumerate(("b1", "CP")):
+            c = s(192 * h, 192 * h + 192)
+            mm(a(b, c), a("N4"), a("M", c), False, True)
+            act(a("T1", c), a(b, c))
+        urgent[0] = False
         for j in range(N):
             ts(a("ind", s(24 * j, 24 * j + 24)), a("b6", t24), float(j), Op.is_equal if j < N - 1 else Op.is_ge)
         scan(a("sc"), a("RM"), a("ind"), 0.0, Op.mult, Op.add)
-        mm(a("b3", t96), a("TM"), a("ind"), False, False)
-        mm(a("b3", t96), a("BD"), a("sc"), False, True)
-        mm(a("b1", full), a("I8"), a("lose"), False, True)
-        mm(a("b2", full), a("N8"), a("lose"), False, True)
-        tt(a("T1"), a("P"), a("b1", full), Op.min)
-        tt(a("prod"), a("ind"), a("b3", t96), Op.mult)
-        for j in range(N):
-            mm(a("b7", t24), I, a("prod", s(24 * j, 24 * j + 24)), False, j == N - 1)
-        tt(a("T2"), a("A"), a("b2", full), Op.min)
-        cp(a("slot"), a("b7", t24))
-        tt(ix(a("W%d" % r), a("slot")), a("T1"), a("T2"), Op.max)
-        send(r)
         tt(a("y"), a("b6", t24), a("ex"), Op.subtract)
+        for m, x in (("TM", "ind"), ("BD", "sc")):
+            for j in range(N):
+                mm(a("b3", s(j + 1, 120, 5)), a(m), a(x, s(24 * j, 24 * j + 24)), False, x == "sc" and j == N - 1)
+        tt(a("T2"), a("AL"), a("b2", full), Op.min)
+        scan(a("pick"), a("R5"), a("b3", s(0, 120)), 0.0, Op.mult, Op.max)
+        cp(a("slot"), a("pick", s(4, 120, 5)))
         tt(a("y2"), a("y"), a("DU"), Op.min)
         ts(a("so"), a("y2"), 512.0, Op.mult)
+        tt(ix(a("W%d" % r), a("slot")), a("T1"), a("T2"), Op.max)
+        send(r)
+        gate[0] = None
+        into = ix(a("Z"), a("so"))
+        op("s", lambda: g.scalar.activation(into["ap"], T.n32[:], Fn.Silu), into, [a("n32")])
 
-    def pay():
-        cp(ix(a("Z"), a("so")), a("n"))
-
-    ts(a("PHI"), a("bil"), -2047.0, Op.add, 1.0 / 8192, Op.mult)
-    names(every, 0)
     open_round(0)
-    add_names(every, 0)
-    compare(CFG["start"])
+    for i, seg in enumerate((home, far)):
+        names(None, seg, 0)
+        add_names(seg, i)
+    compare(CFG["start"], 0)
+    for o in later[CFG["soon"]:]:
+        o["gate"] = len(ops) - 1
     settle(0)
     for r in range(1, RO + 1):
-        mine, land = a("W%d" % (r - 1), s(3 * L, 3 * L + C)), lambda seg: a("LA%d" % (r - 1), cols(seg))
+        mine, land = a("W%d" % (r - 1), s(4 * L, 4 * L + C)), lambda seg: a("LA%d" % (r - 1), cols(seg))
         if r == RO:
             break
-        unpack(mine, own, 0)
-        pay()
-        names(own, 0)
+        names(mine, own, 0)
         open_round(r)
-        for i, (seg, ranks) in enumerate(((near, near_r), (far, far_r))):
-            arrived(r - 1, ranks)
-            unpack(land(seg), seg, 1)
-            names(seg, 1)
-            add_names(far if i else home, i)
-        compare(CFG["later"])
-        act(a("P", cols(own)), mine)
+        urgent[0] = True
+        for k in CFG["prep"]:
+            arrived(r - 1, ranks[k])
+            names(land(segs[k]), segs[k], 1)
+            if k != "x":
+                add_names(home if k == "n" else far, int(k != "n"))
+        urgent[0] = False
+        compare(CFG["later"], r)
         settle(r)
-    for seg, ranks in ((far, far_r), (near, near_r), (own, [])):
-        src, c = land(seg) if ranks else mine, cols(seg)
-        arrived(RO - 1, ranks)
-        unpack(src, seg, 1)
-        ts(a("YE", c), phi(seg), 8192.0, Op.mult, 2047.0, Op.add)
-        for eng, out, name in (("s", T.ya, "AU"), ("y", T.ye, "YE")):
-            for x, y, n in (((0, 16, 112), (112, 0, 16)) if ranks else ((0, 0, 128),)):
+    for k in CFG["prep"][::-1] + "o":
+        seg = segs[k]
+        src, c = land(seg) if ranks[k] else mine, cols(seg)
+        arrived(RO - 1, ranks[k])
+        ts(phi(seg), src, MAGIC, Op.add, -MAGIC, Op.add)
+        tt(a("AU", c), src, phi(seg), Op.subtract)
+        ts(a("YE", c), src, MAGIC, Op.add, 2047.0 - MAGIC, Op.add)
+        act(a("A", c), a("AU", c), scale=512.0, bias=1.0)
+        for eng, out, name in (("s", T.ya, "A"), ("y", T.ye, "YE")):
+            for x, y, n in (((0, 16, 112), (112, 0, 16)) if ranks[k] else ((0, 0, 128),)):
                 dma(eng, out[y:y + n, c], a(name, (x, x + n), c), "out")
-    pay()
-    for i in range(2):
-        dma("ys"[i], T.yz[:, 1024 * i:1024 * i + 1024], a("Z", s(1024 * i, 1024 * i + 1024)), "out")
+    for c in (s(0, 1024), s(1024, W)):
+        act(a("ZB", c), a("Z", c), Fn.Relu, bias=-0.501, scale=1.0 / 32)
+        dma("y", T.yz[:, c], a("ZB", c), "out")
 
     def meet(xs, ys):
         return any(x[0] == y[0] and x[1] & y[1] for x in xs for y in ys)
 
     by = {}
-    for i, o in enumerate(ops):
+    for o in ops:
         o["wait"], o["pre"], o["post"] = [], {}, []
+    for i, o in enumerate(ops):
         cand = set()
         for x in o["rd"] + o["wr"]:
             cand.update(by.get(x[0], []))
@@ -435,6 +489,8 @@ def rank_program(g, core, T, topo):
                 o["pre"][j] = 0
         if o["e"] == "x":
             o["pre"][o["after"]] = o["lag"]
+        elif o["gate"]:
+            o["pre"].setdefault(o["gate"], 0)
         for j in o["pre"]:
             ops[j]["post"].append(o)
         for x in set(x[0] for x in o["rd"] + o["wr"]):
@@ -452,7 +508,8 @@ def rank_program(g, core, T, topo):
         line = sorted(pool[e], key=lambda o: o["rank"])
         pick = None
         for k, o in enumerate(line):
-            if o["ready"] <= t and not any(p["ready"] - t < CFG["patience"].get(e, 1) * (t + o["ns"] - p["ready"]) for p in line[:k]):
+            if o["ready"] <= t and not any(p["ready"] - t < CFG["patience"].get("u" if (p["urgent"] and e != "v") or o["aside"] else e, 1) * (t + o["ns"] - p["ready"])
+                                           for p in line[:k]):
                 pick = o
                 break
         if pick is None:

from concourse.bass import DstId, RemoteDMATransfer
from concourse.mybir import AluOpType as Op, ActivationFunctionType as Fn, AxisListType as Ax

N, L, C, W, RO = 4, 384, 96, 2048, 5
MAGIC = 12582912.0
BIG = 1048576.0
f32, bf, f16, i32, u16 = "float32", "bfloat16", "float16", "int32", "uint16"
CYCLE = 0.83
CFG = {"issue": 100, "pe": 0.45, "gather": 1.56, "scatter": 3.8, "fix": 20, "hop": 200, "dma": 2000, "lag": [2400, 3300, 3300],
       "patience": {"v": 1.2, "s": 0, "t": 0, "u": 3}, "cut": 1536, "banks": "b1 b2 b3", "prep": "nf", "late_c": False, "soon": 0, "ahead": 4, "paced": "", "bw": True, "split": False, "comb": False,
       "start": "Sheg Shce Shac Sh9a Vh02468 Ch02 Vh1357 Ch12 Sfce Sfeg Sfab Sfbc Vf048 Cf04 Vf159 Cf14 Vf26 Cf24 Vf37 Cf34",
       "later": "Socg So8c Vo01234567 Sncg Sn9c Vn012345678 Sfef Sfcd Sfab Sfde Sffg Sfbc Co01 Cn01 Vf02468 Cf02 Vf159 Cf14 Vf37 Cf34"}


def sb(n, d):
    return ("sbuf", [128] + (n if isinstance(n, list) else [n]), d)


SCRATCH = {"PHI": sb([12, 2, 16], f16), "CMP": sb([L, 16], bf), "A32": sb(L, bf), "AL": sb(L, bf), "NS": ("psum", [128, 16, 2, 16], f32),
           "CP": ("psum", [128, 512], f32), "EQ": sb([24, L], bf), "crow0": sb([24, 16], bf), "crow1": sb([24, 16], bf)}
for _d, _l in ((f32, "Z:2432 n32 P NT NK S T1 T2 ab:24 gk:24 xs:24 ex:24 y:24 y2:24 DU:24 q1:24 YE col:8 gcol:8 K:392 U:24 c0:120 R5:120 pick:120 lj:24 lb:24 "
                     "SH32:128 I32:128 la:48 ID:2048 h16:16 w16:16 v16:16 m16:16 wj:8"),
               (bf, "A ZB:2048 wcol:16 AU VB:6144 d n kk:24 e:24 nq:24 ind:96 sc:96 B8:8 WB:144 WW:144 WH:144 U16 M16 "
                    "G8:128 BD:128 BW:128 BJ:128 TM:128 IB:128 NB:128 M I4:128 N4:128 N8:128 NH:128 SH:128 SW:1024 SEL:2048 ones rows:768 RM:96"),
               (i32, "bil r:24 x:24 rk:24 ci:24 rel:24 ri:8 rj:8 rg:8 lq:48"),
               (f16, "XR CC:120"),
               (u16, "OFF xo:24 so:24 slot:24 LS:96")):
    for _n in _l.split():
        SCRATCH[_n.split(":")[0]] = sb(int(_n.split(":")[1]) if ":" in _n else L, _d)
SCRATCH.update(hits=("psum", [128, 32, 16], f32), lose=sb([24, 16], bf))
for _n in ("b1", "b2", "b3", "b6", "b7"):
    SCRATCH[_n] = ("psum", [128, 512], f32)
for _r in range(RO):
    SCRATCH["W%d" % _r] = sb(5 * L, f32)
    SCRATCH["LA%d" % _r] = sb(L, f32)
SEMAPHORES = (["ev", "es", "et", "eg", "acc0", "acc1", "keys", "sent", "out"] + ["l%d" % k for k in range(4)]
              + ["ar%d_%d" % (r, q) for r in range(RO) for q in range(N)])


def rank_program(g, core, T, topo):
    q = T.rank_of(core)
    if q is None:
        return
    ops, aside, urgent, gate = [], [False], [False], [None]
    Q = {"v": g.vector, "s": g.scalar, "t": g.tensor, "g": g, "y": g.sync}

    def a(name, *idx):
        where, shape, kind = SCRATCH[name]
        rows = slice(None)
        if idx and isinstance(idx[0], tuple):
            rows = slice(*idx[0]); idx = idx[1:]
        idx = list(idx) + [slice(None)] * (len(shape) - 1 - len(idx))
        m, size = 1, 1
        for k, n in reversed(list(zip(idx, shape[1:]))):
            rg = range(n)[k] if isinstance(k, slice) else [k]
            m = sum(m << (size * i) for i in rg); size *= n
        return {"ap": T[name][tuple([rows] + idx)], "reg": [(name, 1 if where == "psum" else m)], "ps": where == "psum",
                "n": m.bit_count(), "two": kind in (bf, f16, u16)}

    def s(x, y=None, z=None):
        return slice(x, y, z)

    def ix(win, off):
        return {"ap": win["ap"].indirect(off["ap"]), "reg": win["reg"], "off": off["reg"], "ps": False, "n": 16 * off["n"]}

    def ap(x):
        return x["ap"] if isinstance(x, dict) else x

    def span(eng, out, ins, sem, both):
        if sem:
            return CFG["issue"]
        n, x = out["n"], (ins or [out])[0]
        if eng == "t":
            return max(64, n) * CFG["pe"] * (1 if x["two"] else 4)
        if eng == "g":
            return 150 + 2 * n * CYCLE
        if "off" in out or "off" in x:
            return 60 + n * CYCLE * CFG["scatter" if "off" in out else "gather"]
        per = 1 if eng == "s" else (1 if x["ps"] or ins[1]["ps"] else 2) if both else 0.5 if out["two"] and x["two"] else 1
        return CFG["fix"] + max(64, n * per) * CYCLE

    def op(eng, fn, out, ins, sem=None, both=False):
        rd, wr = [], []
        for x in ins:
            if isinstance(x, dict):
                rd += x["reg"] + x.get("off", [])
                if x["ps"]:
                    wr += [(n, m, "ps") for n, m in x["reg"]]
        if isinstance(out, dict):
            wr += out["reg"]; rd += out.get("off", [])
        ops.append({"e": eng, "fn": fn, "rd": rd, "wr": wr, "sem": sem, "ns": span(eng, out, ins, sem, both), "aside": aside[0],
                    "urgent": urgent[0], "gate": gate[0] if aside[0] else None})

    def tt(out, x, y, o):
        op("v", lambda: g.vector.tensor_tensor(ap(out), ap(x), ap(y), o), out, [x, y], both=True)

    def ts(out, x, s1, o0, s2=None, o1=None):
        if o1 is None:
            op("v", lambda: g.vector.tensor_scalar(ap(out), ap(x), ap(s1), None, o0), out, [x, s1])
        else:
            op("v", lambda: g.vector.tensor_scalar(ap(out), ap(x), ap(s1), ap(s2), o0, o1), out, [x, s1, s2])

    def cp(out, x):
        op("v", lambda: g.vector.tensor_copy(ap(out), ap(x)), out, [x])

    def ms(out, v):
        op("v", lambda: g.vector.memset(ap(out), v), out, [])

    def scan(out, d0, d1, init, o0, o1):
        op("v", lambda: g.vector.tensor_tensor_scan(ap(out), ap(d0), ap(d1), init, o0, o1), out, [d0, d1])

    def act(out, x, f=Fn.Identity, bias=0.0, scale=1.0):
        op("s", lambda: g.scalar.activation(ap(out), ap(x), f, bias=bias, scale=ap(scale)), out, [x, scale])

    def mm(out, lhs, rhs, start, stop):
        op("t", lambda: g.tensor.matmul(ap(out), ap(lhs), ap(rhs), start, stop), out, [lhs, rhs])

    def iota(out, pat, base, cm, flt=True):
        if flt:
            op("g", lambda: g.iota(ap(out), pat, base, cm, allow_small_or_imprecise_dtypes=True), out, [])
        else:
            op("g", lambda: g.iota(ap(out), pat, base, cm), out, [])

    def sel(out, x, pat, cmp_, fill, base, cm):
        op("g", lambda: g.affine_select(ap(out), ap(x), pat, cmp_, fill, base, cm), out, [x])

    def dma(eng, out, x, sem, **kw):
        ins = [x, out] if kw else [x]
        op(eng, lambda: Q[eng].dma_start(ap(out), ap(x), **kw), out, ins, sem)

    scol, wcol = a("col", s(0, 1)), a("wcol", s(0, 1))
    I, NI = a("IB"), a("NB")
    one1 = lambda n: a("ones", (0, 1), s(0, n))
    row = lambda k, n=128: a("rows", (0, 1), s(128 * k, 128 * k + n))
    selk = lambda k: a("SEL", s(128 * k, 128 * k + 128))
    full, t24, t96, z = s(0, L), s(0, 24), s(0, 96), a("Z", s(0, W))

    near_r = [k for k in range(N) if k != q and T.cores[k] in topo.cores_of(core)]
    far_r = [k for k in range(N) if k != q and k not in near_r]
    own, near, far = [(6 * min(k), 6 * max(k) + 6) for k in ([q], near_r, far_r)]
    every, home = (0, 24), (min(own[0], near[0]), max(own[1], near[1]))
    far_r.sort(key=lambda k: topo.die(T.cores[k]) != topo.die(core))
    ranks = {"o": [], "n": near_r, "f": far_r, "x": far_r[:1], "y": far_r[1:]}
    segs = {k: (6 * min(v), 6 * max(v) + 6) for k, v in ranks.items() if v}
    segs.update(a=every, o=own, h=home)
    cols = lambda seg: s(16 * seg[0], 16 * seg[1])
    lists = {12: 0, 6: 12}

    dma("y", a("bil"), T.bills[:], "l0")
    dma("s", a("A"), T.due[:], "l1")
    dma("y", a("ZB"), T.z0[:], "l2")
    op("s", lambda: g.scalar.dma_start(T.wcol[:, 0:1], T.wt[:]), a("wcol"), [], "l3")
    aside[0] = True
    for k in range(0, W, 512):
        act(a("Z", s(k, k + 512)), a("ZB", s(k, k + 512)), Fn.Silu, scale=32.0, bias=16.0)
    ops[-4]["ns"] += 1300
    iota(a("ri"), [[0, 8]], 0, 1, False)
    iota(a("U"), [[16, 24]], 0, 0)
    iota(a("G8"), [[1, 8], [0, 16]], 0, 0)
    iota(a("U16"), [[0, 24], [1, 16]], 0, 0)
    iota(a("K"), [[2048, 392]], 2047, 0)
    for k in range(0, W, 512):
        iota(a("ID", s(k, k + 512)), [[1, 512]], k, 0)
    iota(a("c0"), [[0, 24], [L, 5]], -2049, 0)
    for name, v in (("ones", 1.0), ("B8", BIG), ("WB", 0.0), ("h16", 0.5), ("RM", 1.0)):
        ms(a(name), v)
    ms(a("RM", s(0, 96, 24)), 0.0)
    ms(a("rows", (0, 2), s(128, 256)), 1.0); ms(row(4), -23.0); ms(row(5), 44.5)
    iota(row(1), [[0, 8], [4096, 16]], 0, 0)
    o128 = a("ones", s(0, 128))
    for sh in range(2):
        for h in range(2):
            for h2 in range(2):
                m = a("SW", s(512 * sh + 256 * h + 128 * h2, 512 * sh + 256 * h + 128 * h2 + 128))
                base = 16 * sh - 16 * h2 - 1000 * h
                sel(m, o128, [[-32, 4], [1000, 2], [-1, 16]], Op.is_equal, 0.0, base, 1)
                if sh and not h2:
                    sel(m, m, [[-32, 4], [1000, 2], [-1, 16]], Op.not_equal, 1.0, base - 128, 1)
    sel(a("SH"), o128, [[-1, 128]], Op.is_equal, 0.0, 16, 1)
    sel(a("SH"), a("SH"), [[-1, 128]], Op.not_equal, 1.0, -112, 1)
    ts(a("rg"), a("ri"), 4, Op.arith_shift_right)
    cp(a("gcol"), a("rg"))
    ts(a("BD"), a("G8"), a("gcol", s(0, 1)), Op.is_equal)
    tt(I, a("SW", s(0, 128)), a("SW", s(384, 512)), Op.add)
    sel(a("B8"), a("B8"), [[-16, 8]], Op.is_ge, 0.0, 0, 1)
    sel(a("WB", s(15, 143, 16)), a("B8"), [[16, 8]], Op.is_ge, 0.0, 15, -1)
    sel(a("TM"), a("BD"), [[-1, 128]], Op.is_gt, 0.0, 0, 1)
    ts(a("rj"), a("ri"), 15, Op.bitwise_and)
    cp(scol, a("rj", s(0, 1)))
    ts(a("lj"), a("U"), scol, Op.add)
    ts(a("lb"), a("lj"), 16.0, Op.mult)
    for nu, x in lists.items():
        c, o = s(0, nu), s(x, x + nu)
        ts(a("lq", o), a("lj", c), -(nu - 1) / 2.0, Op.add, 1.0 / nu, Op.mult)
        ts(a("la", o), a("lq", o), 1.0 - 16.0 * nu, Op.mult)
        tt(a("la", o), a("la", o), a("lb", c), Op.add)
        cp(a("LS", o), a("la", o))
    for name, steps in (("crow0", CFG["start"].split()), ("crow1", CFG["later"].split())):
        ms(a(name, (0, 1)), -8 * BIG)
        for k in sorted({st[1] for st in steps if st[0] == "S"}):
            ms(a(name, (0, 1), s(*segs[k]), s(min(int(st[2], 16) for st in steps if st[:2] == "S" + k), 16)), 0.0)
    ts(a("M16"), a("U16"), scol, Op.is_equal, -2.0, Op.mult)
    ts(a("v16"), a("U", s(0, 16)), 1.0 / 16, Op.mult, scol, Op.is_equal)
    ts(a("m16"), a("v16"), 4096.0, Op.mult)
    scan(a("w16"), a("h16"), a("h16"), 0.5, Op.mult, Op.min)
    tt(a("w16"), a("w16"), a("v16"), Op.mult)
    op("v", lambda: g.vector.tensor_reduce(T.wj[:, 0:1], T.w16[:], Ax.X, Op.add), a("wj"), [a("w16")])
    ts(a("BJ"), a("BD"), a("wj", s(0, 1)), Op.mult)
    ts(a("WW"), a("WB"), wcol, Op.mult, 1.0 / BIG, Op.mult)
    ts(a("BW"), a("BD"), wcol, Op.mult)
    ts(a("DU"), a("lj"), float(W), Op.add, 1.0 / 512, Op.mult)
    cp(a("CC"), a("c0"))
    cp(a("CC", s(0, 120, 5)), a("lj"))
    ms(a("R5"), 1.0)
    ms(a("R5", s(0, 120, 5)), 0.0)
    ts(a("NB"), a("IB"), -1.0, Op.mult)
    act(a("NH"), a("SH"), scale=-1.0)
    act(a("SH32"), a("SH"))
    act(a("I4"), I, scale=-4096.0)
    act(a("N4"), I, scale=-4.0)
    act(a("N8"), I, scale=-131072.0)
    act(a("WH"), a("WB"), scale=0.5 / BIG)
    act(a("TM"), a("TM"), scale=-1.0)
    sel(a("TM"), a("TM"), [[-1, 128]], Op.not_equal, 2048.0, 0, 1)
    for k in range(16):
        act(selk(k), a("BD"), scale=a("m16", s(k, k + 1)))
    later = [o for o in ops if o["aside"] and (o["wr"][0][0] not in ("A32", "SEL") if o["e"] == "s" else
                                               o["wr"][0][0] in ("WW", "M16", "CC"))]
    for o in ops:
        o["aside"] = o["aside"] and o["wr"][0][0] not in ("ri", "U", "G8", "rg", "gcol", "BD", "rj", "col", "v16", "m16")
    for r in range(RO):
        for j in range(N):
            iota(a("W%d" % r, s(L * j + L, L * j + L + C)), [[0, C]], 0, 0)
    aside[0] = False

    def phi(seg):
        return a("PHI", s(seg[0] // 2, seg[1] // 2))

    def names(src, seg, sh):
        b, c, nu = s(seg[0] // 2, seg[1] // 2), cols(seg), seg[1] - seg[0]
        if src:
            ts(phi(seg), src, MAGIC, Op.add, -MAGIC, Op.add)
        else:
            ts(phi(seg), a("bil", c), -2047.0, Op.add)
        for h2 in range(2):
            for h in range(2):
                k = 512 * sh + 256 * h + 128 * h2
                mm(a("NS", b, h2), a("SW", s(k, k + 128)), a("PHI", b, h), h == 0, h == 1)
        if src and seg == far:
            mm(a("b7", c), a("SH32"), src, True, False)
            mm(a("b7", c), a("NH"), phi(seg), False, True)
        elif src:
            tt(a("AU", c), src, phi(seg), Op.subtract)
            if sh:
                mm(a("b7", c), a("SH"), a("AU", c), True, True)
        if src:
            act(a("A32", c), a("b7" if sh else "AU", c), scale=16384.0, bias=32.0)
        op("v", lambda: g.vector.transpose(ap(a("NT", c)), ap(a("NS", b))), a("NT", c), [a("NS", b)])
        ts(a("OFF", c), ix(a("NT", c), a("LS", s(lists[nu], lists[nu] + nu))), 2047.0, Op.add)

    bank = [0]

    def fetch(out, off, r):
        if r:
            act(out, ix(z, off), bias=-16.0)
        else:
            act(out, ix(a("ZB"), off))

    def compare(plan_, r):
        steps, signs = plan_.split(), []
        bank[0] = 0
        for i, st in enumerate(steps):
            seg, p0, p1 = segs[st[1]], int(st[2], 17), int(st[3:4] or "0", 17)
            nu, c, m = seg[1] - seg[0], cols(seg), p1 - p0
            w, due = 16 * nu, a("A32" if r else "A", c)
            off = lambda x, y: a("OFF", s(16 * seg[0] + nu * x, 16 * seg[0] + nu * y))
            vb = lambda x, y: a("VB", s(256 * seg[0] + w * x, 256 * seg[0] + w * y))
            if st[0] == "V":
                for p in [int(x, 16) for x in st[2:]]:
                    tt(a("CMP", c, p), ix(z if r else a("ZB"), off(p, p + 1)), due, Op.is_ge)
            elif st[0] == "S":
                nm = CFG["banks"].split()[bank[0] % len(CFG["banks"].split())]
                bank[0] += 1
                fetch(vb(p0, p1), off(p0, p1), r)
                if len(signs) > 1 and st[1] in CFG["paced"]:
                    ops[-1]["gate"] = signs[-2]
                for k in range(m):
                    mm(a(nm, s(k, w * m, m)), NI, due, k == 0, False)
                for k in range(m):
                    mm(a(nm, s(k, w * m, m)), I, vb(p0 + k, p0 + k + 1), False, k == m - 1)
                act(a("CMP", c, s(p0, p1)), a(nm, s(0, w * m)), Fn.Sign, bias=0.25)
                signs.append(len(ops) - 1)
            else:
                for k in range(16):
                    last = not any(x[0] == "C" and (x[1] == "f") == (st[1] == "f") for x in steps[i + 1:])
                    mm(a("CP" if st[1] == "f" else "b6", s(16 * seg[0] + p0, 16 * seg[1], p1)), a("WB", s(15 - k, 143 - k)),
                       a("CMP", s(16 * seg[0] + k, 16 * seg[1], 16), s(p0, 16, p1)), False, last and k == 15)

    def open_round(r):
        aside[0] = True
        for b, seg in (("b6", home), ("CP", far)):
            mm(a(b, cols(seg)), one1(128), a("crow1" if r else "crow0", (0, 1), s(*seg)), True, False)
        dma("y", a("NK"), a("K", s(1, L + 1)), "keys")
        aside[0] = False

    def add_names(seg, i):
        dma("g", a("NK", cols(seg)), a("NT", cols(seg)), "acc%d" % i, accum_op=Op.add)

    def arrived(r, ranks):
        for src in ranks:
            ops.append({"e": "x", "rd": [], "wr": a("LA%d" % r, s(C * src, C * src + C))["reg"], "sem": "ar%d_%d" % (r, src),
                        "n": len(few) // (1 if CFG["split"] or src in near_r else 2), "ns": 0, "urgent": False, "after": sends[r], "aside": False,
                        "lag": CFG["lag"][(near_r + far_r).index(src)]})

    few = topo.engines(core, T.cores[far_r[0]])
    rest = [e for e in topo.engines(core, T.cores[near_r[0]]) if e not in few]
    sent, sends = [0], []

    def send(r):
        sends.append(len(ops))
        for dests in ((far_r[:1] + near_r, far_r[1:]) if CFG["split"] else (far_r + near_r,)):
            trs, rd = [], []
            for k in dests:
                j, eng = (k - q - 1) % N, few if k in far_r else rest
                if not CFG["split"] and k in far_r:
                    eng = few[far_r.index(k)::2] if CFG["comb"] else few[4 * far_r.index(k):4 * far_r.index(k) + 4]
                rid, pid = topo.addr(T.cores[k], core)
                src = a("W%d" % r, s(L * j + L, L * j + L + C)); rd.append(src)
                trs.append(RemoteDMATransfer(dst_ids=[DstId(rid=rid, pnc=pid)], dma_engine_mask=sum(1 << e for e in eng),
                                             remote_sem=T.sem["ar%d_%d" % (r, q)], src=ap(src),
                                             dst=T["LA%d" % r][:, C * q:C * q + C]))
                sent[0] += len(eng)
            op("g", lambda trs=trs: g.remote_dma_fused(trs, local_sem=T.sem.sent), None, rd, "none")

    def settle(r):
        gate[0] = len(ops) - 1
        for b, seg in (("CP", far), ("b6", home)):
            c, u, x = cols(seg), s(*seg), 16 * seg[0]
            scan(a("S", c), a(b, c), a("NK", c), 0.0, Op.max, Op.min)
            tt(a("r", u), a("S", s(x + 15, x + 192, 16)), a("K", s(x, x + 192, 16)), Op.max)
            ts(a("x", u), a("r", u), W - 1, Op.bitwise_and)
            cp(a("xo", u), a("x", u))
            ts(a("XR", c), ix(a("ID"), a("xo", u)), 1.0 / 512, Op.mult)
            ts(a("xs", u), a("x", u), 1.0 / 512, Op.mult)
        ts(a("rk"), a("r"), 11, Op.arith_shift_right)
        tt(a("kk"), a("U"), a("rk"), Op.subtract)
        aside[0] = True
        mm(a("b3", full), NI, a("A32" if r else "A"), True, False)
        mm(a("b7", t24), row(4), row(5, 24), True, False)
        aside[0] = False
        for seg in (home, far):
            fetch(a("d", cols(seg)), a("xo", s(*seg)), r)
            mm(a("b3", cols(seg)), I, a("d", cols(seg)), False, seg == far)
        act(a("n"), a("b3", full), Fn.Relu, scale=1.0 / 32 if r else 1.0)
        mm(a("b7", t24), a("I4"), a("kk"), False, False)
        aside[0] = CFG["late_c"]
        for k in range(16):
            mm(a("b7", t24), a("WW", s(15 - k, 143 - k)), a("n", s(k, L, 16)), False, k == 15)
        act(a("q1"), a("b7", t24), bias=MAGIC, scale=1.0 / 2048)
        act(a("nq"), a("q1"), bias=(MAGIC - 1) / 2, scale=-0.5)
        aside[0] = True
        act(a("n32"), a("b3", full), Fn.Relu, bias=16.0, scale=1.0 if r else 32.0)
        act(a("AL"), a("A32" if r else "A"), scale=1.0 / (16384 if r else 512), bias=-1.0 / 512)
        mm(a("NS", s(0, 12)), a("rows", (0, 2), s(128, 256)), a("ones", (0, 2)), True, False)
        for k in range(16):
            mm(a("NS", s(0, 12), s(0, 2), k), selk(k), a("kk"), False, False)
        act(a("ab"), a("kk"), Fn.Abs, bias=-68.0, scale=-8.0)
        act(a("gk"), a("ab"), bias=58.0, scale=-1.0)
        ts(a("ci"), a("b7", t24), 1023.5 + 3 - q, Op.add)
        for b, half in (("b1", (0, 12)), ("CP", (12, 24))):
            mm(a(b, cols(half)), I, a("AL", cols(half)), True, False)
            for seg in ([far] if half == far else [own, near]):
                mm(a(b, cols(seg)), a("SH") if r and seg != own else I, phi(seg), False, False)
        ts(a("rel"), a("ci"), N - 1, Op.bitwise_and)
        tt(a("e"), a("rel"), a("gk"), Op.min)
        tt(a("ex"), a("e"), a("xs"), Op.subtract)
        mm(a("hits", t24), a("BJ"), a("M16"), True, False)
        mm(a("b2", full), a("rows", (0, 2), s(128, 256)), a("ones", (0, 2)), True, False)
        mm(a("b2", full), a("BW"), a("n"), False, False)
        for k in range(16):
            mm(a("b2", s(k, L, 16)), selk(k), a("nq"), False, False)
        mm(a("b2", full), I, a("AL"), False, False)
        mm(a("b3", s(0, 120)), I, a("CC"), True, False)
        aside[0] = False
        n = CFG["ahead"]
        pairs = ([(u, u, 12) for u in range(n)] + [(u, 12, 24) for u in range(n)] + [(u, u, 24) for u in range(n, 24)] if home[0] == 0
                 else [(u, u, 24) for u in list(range(12, 12 + n)) + list(range(12)) + list(range(12 + n, 24))])
        diag = {17: s(0, 18), 23: s(18, 24)}
        for u, x, y in pairs:
            ts(a("EQ", u, s(16 * (x - u), 16 * (y - u))), a("XR", s(16 * x, 16 * y)), a("xs", s(u, u + 1)), Op.is_equal)
            x = max(x, u + 1)
            if x < y:
                mm(a("hits", s(x, y)), a("BD"), a("EQ", u, s(16 * (x - u), 16 * (y - u))), False, False)
            if u in diag and y == 24:
                mm(a("hits", diag[u]), a("BJ"), a("EQ", diag[u], s(0, 16)), False, u == pairs[-1][0])
        for c in (s(0, 8), s(8, 16)):
            ts(a("lose", t24, c), a("hits", t24, c), 0.0, Op.is_ge)
        for k in range(16):
            mm(a("b6", t24), a("WH", s(15 - k, 143 - k)), a("lose", t24, k), k == 0, False)
        mm(a("b6", t24), I, a("e"), False, True)
        urgent[0] = True
        mm(a("NS", s(0, 12)), a("N8"), a("lose"), False, True)
        for h in range(2):
            act(a("M", s(192 * h, 192 * h + 192)), a("NS", s(6 * h, 6 * h + 6)), Fn.Relu, bias=2048.0)
        mm(a("b2", full), a("N8"), a("lose"), False, True)
        for h, b in enumerate(("b1", "CP")):
            c = s(192 * h, 192 * h + 192)
            mm(a(b, c), a("N4"), a("M", c), False, True)
            act(a("T1", c), a(b, c))
        urgent[0] = False
        for j in range(N):
            ts(a("ind", s(24 * j, 24 * j + 24)), a("b6", t24), float(j), Op.is_equal if j < N - 1 else Op.is_ge)
        scan(a("sc"), a("RM"), a("ind"), 0.0, Op.mult, Op.add)
        tt(a("y"), a("b6", t24), a("ex"), Op.subtract)
        for m, x in (("TM", "ind"), ("BD", "sc")):
            for j in range(N):
                mm(a("b3", s(j + 1, 120, 5)), a(m), a(x, s(24 * j, 24 * j + 24)), False, x == "sc" and j == N - 1)
        tt(a("T2"), a("AL"), a("b2", full), Op.min)
        scan(a("pick"), a("R5"), a("b3", s(0, 120)), 0.0, Op.mult, Op.max)
        cp(a("slot"), a("pick", s(4, 120, 5)))
        tt(a("y2"), a("y"), a("DU"), Op.min)
        ts(a("so"), a("y2"), 512.0, Op.mult)
        tt(ix(a("W%d" % r), a("slot")), a("T1"), a("T2"), Op.max)
        send(r)
        gate[0] = None
        into = ix(a("Z"), a("so"))
        op("s", lambda: g.scalar.activation(into["ap"], T.n32[:], Fn.Silu), into, [a("n32")])

    open_round(0)
    for i, seg in enumerate((home, far)):
        names(None, seg, 0)
        add_names(seg, i)
    compare(CFG["start"], 0)
    for o in later[CFG["soon"]:]:
        o["gate"] = len(ops) - 1
    settle(0)
    for r in range(1, RO + 1):
        mine, land = a("W%d" % (r - 1), s(4 * L, 4 * L + C)), lambda seg: a("LA%d" % (r - 1), cols(seg))
        if r == RO:
            break
        names(mine, own, 0)
        open_round(r)
        urgent[0] = True
        for k in CFG["prep"]:
            arrived(r - 1, ranks[k])
            names(land(segs[k]), segs[k], 1)
            if k != "x":
                add_names(home if k == "n" else far, int(k != "n"))
        urgent[0] = False
        compare(CFG["later"], r)
        settle(r)
    for k in CFG["prep"][::-1] + "o":
        seg = segs[k]
        src, c = land(seg) if ranks[k] else mine, cols(seg)
        arrived(RO - 1, ranks[k])
        ts(phi(seg), src, MAGIC, Op.add, -MAGIC, Op.add)
        tt(a("AU", c), src, phi(seg), Op.subtract)
        ts(a("YE", c), src, MAGIC, Op.add, 2047.0 - MAGIC, Op.add)
        act(a("A", c), a("AU", c), scale=512.0, bias=1.0)
        for eng, out, name in (("s", T.ya, "A"), ("y", T.ye, "YE")):
            for x, y, n in (((0, 16, 112), (112, 0, 16)) if ranks[k] else ((0, 0, 128),)):
                dma(eng, out[y:y + n, c], a(name, (x, x + n), c), "out")
    for c in (s(0, 1024), s(1024, W)):
        act(a("ZB", c), a("Z", c), Fn.Relu, bias=-0.501, scale=1.0 / 32)
        dma("y", T.yz[:, c], a("ZB", c), "out")

    def meet(xs, ys):
        return any(x[0] == y[0] and x[1] & y[1] for x in xs for y in ys)

    by = {}
    for o in ops:
        o["wait"], o["pre"], o["post"] = [], {}, []
    for i, o in enumerate(ops):
        cand = set()
        for x in o["rd"] + o["wr"]:
            cand.update(by.get(x[0], []))
        for j in cand:
            p = ops[j]
            real = [x for x in p["wr"] if len(x) == 2]
            same = p["e"] == o["e"] and p["sem"] is None and o["sem"] is None
            if same:
                hit = o["e"] != "t" and (meet(o["rd"] + o["wr"], real) or meet([x for x in o["wr"] if len(x) == 2], p["rd"]))
            else:
                hit = meet(o["rd"], real) or meet(o["wr"], p["rd"] + p["wr"])
            if hit and p["sem"] != "none" and o["e"] != "x":
                o["wait"].append(p)
                o["pre"][j] = CFG["hop"] + (CFG["dma"] if p["sem"] and p["e"] != "x" else 0)
            elif same and o["e"] == "t" and meet(o["wr"], p["wr"]):
                o["pre"][j] = 0
        if o["e"] == "x":
            o["pre"][o["after"]] = o["lag"]
        elif o["gate"]:
            o["pre"].setdefault(o["gate"], 0)
        for j in o["pre"]:
            ops[j]["post"].append(o)
        for x in set(x[0] for x in o["rd"] + o["wr"]):
            by.setdefault(x, []).append(i)

    for i, o in reversed(list(enumerate(ops))):
        o["rank"] = (min([p["rank"] for p in o["post"]] + [len(ops)]) - 1e-4) if o["aside"] else i
        o["left"], o["ready"], o["no"] = len(o["pre"]), 0, i
    pool, free, done = {e: [] for e in "vstgyx"}, {e: 0 for e in "vstgyx"}, []
    for o in ops:
        if not o["left"]:
            pool[o["e"]].append(o)
    while len(done) < len(ops):
        t, e = min((max(free[e], min(o["ready"] for o in pool[e])), e) for e in pool if pool[e])
        line = sorted(pool[e], key=lambda o: o["rank"])
        pick = None
        for k, o in enumerate(line):
            if o["ready"] <= t and not any(p["ready"] - t < CFG["patience"].get("u" if (p["urgent"] and e != "v") or o["aside"] else e, 1) * (t + o["ns"] - p["ready"])
                                           for p in line[:k]):
                pick = o
                break
        if pick is None:
            free[e] = min(o["ready"] for o in line if o["ready"] > t)
            continue
        pool[e].remove(pick)
        pick["t"], free[e] = t, t + pick["ns"]
        for o in pick["post"]:
            o["left"] -= 1
            o["ready"] = max(o["ready"], free[e] + o["pre"][pick["no"]])
            if not o["left"]:
                pool[o["e"]].append(o)
        done.append(pick)
    ops = done

    seen = {e: {} for e in "vstgyx"}
    for i, o in enumerate(ops):
        o["i"], o["dep"] = i, {}
        for p in o["wait"]:
            key = p["sem"] or "e" + p["e"]
            if p["i"] > max(seen[o["e"]].get(key, -1), o["dep"].get(key, -1)):
                o["dep"][key] = p["i"]
        seen[o["e"]].update(o["dep"])
        for j in o["dep"].values():
            ops[j]["sig"] = True
    total = {}
    for o in ops:
        key = o["sem"] or "e" + o["e"]
        if o["e"] == "x":
            total[key] = o["at"] = o["n"]
            continue
        for k, j in o["dep"].items():
            Q[o["e"]].wait_ge(T.sem[k], ops[j]["at"])
        ins = o["fn"]()
        if key == "none":
            continue
        if o["sem"] or o.get("sig"):
            n = 16 if o["sem"] else 1
            ins.then_inc(T.sem[key], n)
            total[key] = o["at"] = total.get(key, 0) + n
    total["sent"] = sent[0]
    for k, n in total.items():
        g.wait_ge(T.sem[k], n)
